import numpy as np
import ml_dtypes


def mxq(x, axis, fmt="e4m3"):
    dtype, down = {"e4m3": (ml_dtypes.float8_e4m3fn, 7), "e5m2": (ml_dtypes.float8_e5m2, 14)}[fmt]
    v = np.moveaxis(np.asarray(x, np.float32).astype(ml_dtypes.bfloat16).astype(np.float64), axis, -1)
    blocks = v.reshape(v.shape[:-1] + (-1, 32))
    amax = np.abs(blocks).max(-1, keepdims=True)
    byte = np.maximum(np.where(amax > 0, np.frexp(amax)[1] - 1 + 127, 0) - down, 1)
    scale = np.exp2(byte - 127.0)
    codes = (blocks / scale).astype(np.float32).astype(dtype).astype(np.float64)
    return np.moveaxis((codes * scale).reshape(v.shape), -1, axis)


WIDE = False


def mx_kscale(k):
    if not WIDE:
        return np.ones(k)
    levels = np.array([10, -10, 5, -5, 0])
    if k % 512:
        return np.exp2(np.random.permutation(np.resize(levels, k // 32))).repeat(32)
    a = np.empty((k // 512, 16))
    for p in range(k // 512):
        a[p, :8] = np.random.permutation(np.resize(levels, 8))
        for g in range(8):
            far = levels[np.abs(levels - a[p, g]) >= 10]
            a[p, g + 8] = far[np.random.randint(len(far))]
    return np.exp2(a.ravel()).repeat(32)


BF16 = ml_dtypes.bfloat16


def bf(x):
    return np.asarray(x, np.float32).astype(BF16)


def f64(x):
    return np.asarray(x).astype(np.float64)


T, NB, K, F = 6144, 1, 512, 1024
D = NB * K


def draw0():
    s, t = mx_kscale(K), mx_kscale(K)
    r = mx_kscale(D).reshape(NB, K)
    x = np.random.standard_normal((T, NB, K)) * s
    a = 0.5 * np.random.standard_normal((NB, K, K)) / np.sqrt(K)
    w0 = np.random.standard_normal((NB, K, F)) / np.sqrt(D) / t[None, :, None]
    p = (1.0 + 0.1 * np.random.standard_normal((NB, K))) / s
    q = (1.0 + 0.1 * np.random.standard_normal((NB, K))) * t
    gu = (1.0 + 0.1 * np.random.standard_normal((NB, K))) * r
    gv = (1.0 + 0.1 * np.random.standard_normal((NB, K))) / r
    return {"x": bf(x), "a": bf(a), "w0": bf(w0), "p": bf(p), "q": bf(q), "gu": bf(gu), "gv": bf(gv)}


def identity_plus_skew(a):
    return a - a.transpose(0, 2, 1) + np.eye(a.shape[-1])[None, :, :]


def core(x, a, w0, p, q, gu, gv):
    e = identity_plus_skew(f64(a))

    e1 = f64(p)[:, :, None] * e
    e2 = e * f64(q)[:, None, :]

    xb = f64(x).transpose(1, 0, 2)
    u = mxq(xb, 2, "e4m3") @ mxq(e1, 1, "e4m3")

    v = mxq(e2, 2, "e4m3") @ mxq(f64(w0), 1, "e4m3")

    ug = (u.transpose(1, 0, 2) * f64(gu)[None, :, :]).reshape(T, D)

    vg = (v * f64(gv)[:, :, None]).reshape(D, F)

    return mxq(ug, 1, "e4m3") @ mxq(vg, 0, "e4m3")


def e4m3fn_bytes(y):
    return np.clip(np.asarray(y, np.float64), -448.0, 448.0).astype(np.float32).astype(ml_dtypes.float8_e4m3fn).view(np.uint8)


def e4m3fn_values(b):
    return np.asarray(b, np.uint8).view(ml_dtypes.float8_e4m3fn).astype(np.float64)


def setup_inputs():
    d = draw0()
    x0 = np.asarray(d['x']).astype(np.float64)
    s = (np.max(np.abs(x0), axis=(0, 1), keepdims=True) / 448.0).astype(np.float32)
    out = {}
    for k, v in d.items():
        if k == 'x':
            out['x_bytes'] = e4m3fn_bytes(x0 / s.astype(np.float64))
            out['x_scale'] = s
        else:
            out[k] = v
    return out


def reference(x_bytes, x_scale, a, w0, p, q, gu, gv):
    return core(e4m3fn_values(x_bytes) * x_scale.astype(np.float64), a, w0, p, q, gu, gv)

@@ -1,0 +1,340 @@
+from contextlib import ExitStack
+
+import concourse.mybir as mybir
+from concourse.masks import make_identity
+
+T, K, F = 6144, 512, 1024
+FLOPS = 2 * T * K * K + 2 * K * K * F + 2 * T * K * F
+
+F32 = mybir.dt.float32
+BF16 = mybir.dt.bfloat16
+U32 = mybir.dt.uint32
+U8 = mybir.dt.uint8
+FP8 = mybir.dt.float8_e4m3fn
+FP8X4 = mybir.dt.float8_e4m3fn_x4
+MULT = mybir.AluOpType.mult
+COPY = mybir.ActivationFunctionType.Copy
+
+P = 128
+PACK = 4
+TILES = 4
+BATCH = P * TILES
+NB = T // BATCH
+HALF = F // 2
+
+
+def tile_cayleyneumannorthogonallinear_t_kernel(tc, x_bytes, x_scale, a, w0, p, q, gu, gv, out):
+    nc = tc.nc
+    x_v = x_bytes.rearrange("(b p q) o k -> p b (q o k)", p=P, q=TILES)
+    a_v = a.rearrange("o (m t) k -> (o m) t k", t=PACK)
+    w_v = w0.rearrange("o (m t) f -> (o m) t f", t=PACK)
+    out_v = out.rearrange("(b p q) f -> b p q f", p=P, q=TILES)
+
+    with ExitStack() as ctx:
+        keep = ctx.enter_context(tc.tile_pool(name="keep", bufs=1))
+        stage = ctx.enter_context(tc.tile_pool(name="stage", bufs=3))
+        outs = ctx.enter_context(tc.tile_pool(name="outs", bufs=8))
+        ps_x = ctx.enter_context(tc.psum_pool(name="ps_x", bufs=2))
+        ps_u = ctx.enter_context(tc.psum_pool(name="ps_u", bufs=2))
+        ps_o = ctx.enter_context(tc.psum_pool(name="ps_o", bufs=4))
+        ctx.enter_context(tc.manual_schedule())
+
+        s4 = keep.tile([P, PACK], F32, name="s4")
+        q4 = keep.tile([P, PACK], BF16, name="q4")
+        p4 = keep.tile([P, PACK], BF16, name="p4")
+        gv4 = keep.tile([P, PACK], BF16, name="gv4")
+        gu4 = keep.tile([P, PACK], BF16, name="gu4")
+        nc.scalar.dma_start(out=s4[:], in_=x_scale.rearrange("a o (n m) -> (a o n) m", m=PACK))
+        xb = {}
+
+        def load_x(b0, n):
+            t = keep.tile([P, n, TILES * K], U8, name="x_codes_%d" % b0)
+            nc.sync.dma_start(out=t[:], in_=x_v[:, b0 : b0 + n, :])
+            for i in range(n):
+                xb[b0 + i] = (t, i)
+
+        load_x(0, 1)
+        for vec, t in ((q, q4), (p, p4), (gv, gv4), (gu, gu4)):
+            nc.scalar.dma_start(out=t[:], in_=vec.rearrange("o (n t) -> (o n) t", t=PACK))
+        a4 = keep.tile([P, PACK, K], BF16, name="a4")
+        nc.sync.dma_start(out=a4[:], in_=a_v)
+        w4 = []
+        for h in range(2):
+            t = keep.tile([P, PACK, HALF], BF16, name="w4_%d" % h)
+            nc.sync.dma_start(out=t[:], in_=w_v[:, :, h * HALF : (h + 1) * HALF])
+            w4.append(t)
+            if h == 0:
+                load_x(1, 1)
+        for b0 in range(2, NB, 2):
+            load_x(b0, 2)
+
+        ident = keep.tile([P, P], F32, name="ident")
+        make_identity(nc, ident[:])
+        eye = keep.tile([P, P], BF16, name="eye")
+        nc.vector.tensor_copy(out=eye[:], in_=ident[:])
+        neg = keep.tile([P, P], BF16, name="neg")
+        nc.vector.tensor_scalar(out=neg[:], in0=ident[:], scalar1=-1.0, scalar2=None, op0=MULT)
+        p4f = keep.tile([P, PACK], F32, name="p4f")
+        gv4f = keep.tile([P, PACK], F32, name="gv4f")
+        warm = keep.tile([P, 1], F32, name="warm")
+        nc.vector.memset(warm[:], 1.0)
+        warm2 = keep.tile([P, 1], F32, name="warm2")
+        nc.scalar.activation(out=warm2[:], in_=warm[:], func=COPY, scale=2.0)
+
+        bc = ps_x.tile([P, PACK, P], F32, name="bc", tag="xt")
+        for m in range(PACK):
+            nc.tensor.transpose(bc[:, m, :], s4[:, m : m + 1].to_broadcast([P, P]), ident[:])
+        sc = keep.tile([P, 2, P, PACK], F32, name="sc")
+        nc.vector.tensor_copy(out=sc[:, 0, :, :], in_=bc[:].rearrange("p m n -> p n m"))
+        nc.scalar.copy(out=sc[:, 1, :, :], in_=bc[:].rearrange("p m n -> p n m"))
+        sc_flat = sc[:].rearrange("p r n m -> p (r n m)")
+
+        xw, xg, xq, ub, ug, uq, xt = {}, {}, {}, {}, {}, {}, {}
+
+        def widen(b, h):
+            if b >= NB:
+                return
+            if h == 0:
+                xw[b] = stage.tile([P, TILES * K], BF16, name="xw", tag="xw")
+            t, i = xb[b]
+            cols = slice(h * 2 * K, (h + 1) * 2 * K)
+            nc.vector.tensor_tensor(out=xw[b][:, cols], in0=t[:, i, cols].bitcast(FP8), in1=sc_flat, op=MULT)
+
+        def turn(b, h):
+            if b >= NB:
+                return
+            bank = ps_x.tile([P, 2, 2, P], F32, name="xt", tag="xt")
+            xt[b, h] = bank
+            for i in range(2):
+                base = (2 * h + i) * K
+                words = xw[b][:, base : base + K].bitcast(F32)
+                for u in range(2):
+                    nc.tensor.transpose(bank[:, i, u, :], words[:, u : K // 2 : 2], ident[:])
+
+        def gather_k(b, h):
+            if b >= NB:
+                return
+            if h == 0:
+                xg[b] = stage.tile([P, BATCH * PACK], BF16, name="xg", tag="xg", align_bytes=64)
+            words = xg[b][:, h * 2 * K : (h + 1) * 2 * K].bitcast(F32)
+            nc.scalar.copy(out=words.rearrange("p (i r u) -> p i r u", i=2, u=2), in_=xt[b, h][:].rearrange("p i u r -> p i r u"))
+
+        def codes(name, pool, width):
+            c = pool.tile([P, width], U32, name=name + "_c", tag=name + "_c", align_bytes=64)
+            s = pool.tile([P, width], U8, name=name + "_s", tag=name + "_s", align_bytes=64)
+            return c, s
+
+        def quant(dst, cols, src):
+            nc.vector.quantize_mx(out=dst[0][:, cols].bitcast(FP8X4), scales=dst[1][:, cols], in_=src)
+
+        def quant_x(k):
+            b, h = divmod(k, 2)
+            if b < NB:
+                if h == 0:
+                    xq[b] = codes("xq", stage, BATCH)
+                quant(xq[b], slice(h * 2 * P, (h + 1) * 2 * P), xg[b][:, h * 2 * K : (h + 1) * 2 * K])
+
+        def mx(dst, l, lc, r, rc):
+            nc.tensor.matmul_mx(
+                out=dst, lhsT=l[0][:, lc].bitcast(FP8X4), lhsT_scale=l[1][:, lc],
+                rhs=r[0][:, rc].bitcast(FP8X4), rhs_scale=r[1][:, rc], start=True, stop=True,
+            )
+
+        def first(b, i):
+            if b >= NB:
+                return
+            bank = ps_u.tile([P, PACK, P], F32, name="u", tag="u")
+            ub[b, i] = bank
+            for t in range(PACK):
+                mx(bank[:, t, :], e1q, slice(t * P, (t + 1) * P), xq[b], slice(i * P, (i + 1) * P))
+
+        def gain(b, i):
+            if b >= NB:
+                return
+            if i == 0:
+                ug[b] = stage.tile([P, BATCH, PACK], BF16, name="ug", tag="ug", align_bytes=64)
+                uq[b] = codes("uq", stage, BATCH)
+            nc.vector.tensor_tensor(
+                out=ug[b][:, i * P : (i + 1) * P, :], in0=ub[b, i][:].rearrange("p t r -> p r t"),
+                in1=gu4[:].unsqueeze(1).to_broadcast([P, P, PACK]), op=MULT,
+            )
+
+        def quant_u(b, i0, n):
+            if b < NB:
+                cols = slice(i0 * P, (i0 + n) * P)
+                quant(uq[b], cols, ug[b][:, cols, :].rearrange("p n t -> p (n t)"))
+
+        ob, res = {}, {}
+
+        def second(b, i, h):
+            if b < 0:
+                return
+            bank = ps_o.tile([P, HALF], F32, name="o", tag="o")
+            ob[b, i, h] = bank
+            mx(bank[:], uq[b], slice(i * P, (i + 1) * P), vgq[h], slice(0, HALF))
+
+        def leave(b, i, h, eng):
+            if b < 0:
+                return
+            if (b, i) not in res:
+                res[b, i] = outs.tile([P, F], F32, name="res", tag="res")
+            cols = slice(h * HALF, (h + 1) * HALF)
+            if eng == "V":
+                nc.vector.tensor_copy(out=res[b, i][:, cols], in_=ob[b, i, h][:])
+            else:
+                nc.scalar.copy(out=res[b, i][:, cols], in_=ob[b, i, h][:])
+
+        def store(b, i):
+            if b >= 0:
+                nc.sync.dma_start(out=out_v[b, :, i, :], in_=res[b, i][:])
+
+        def skew(dst, t_out, t_in, first_eye, second_eye):
+            nc.tensor.matmul(dst, lhsT=a4[:, t_out, t_in::PACK], rhs=first_eye[:], start=True, stop=False)
+            nc.tensor.matmul(dst, lhsT=second_eye[:], rhs=a4[:, t_in, t_out::PACK], start=False, stop=(t_in != t_out))
+            if t_in == t_out:
+                nc.tensor.matmul(dst, lhsT=eye[:], rhs=eye[:], start=False, stop=True)
+
+        e2g = keep.tile([P, PACK, P, PACK], BF16, name="e2g", align_bytes=64)
+        e2q = codes("e2q", keep, K)
+        e1p = keep.tile([P, PACK, K], BF16, name="e1p")
+        e1g = keep.tile([P, K, PACK], BF16, name="e1g", align_bytes=64)
+        e1q = codes("e1q", keep, K)
+        wg = [keep.tile([P, HALF, PACK], BF16, name="wg_%d" % h, align_bytes=64) for h in range(2)]
+        wq = [codes("wq%d" % h, keep, HALF) for h in range(2)]
+        vgb = [keep.tile([P, HALF, PACK], BF16, name="vgb_%d" % h, align_bytes=64) for h in range(2)]
+        vgq = [codes("vgq%d" % h, keep, HALF) for h in range(2)]
+        eb, vb = {}, {}
+        FULL = slice(0, 512)
+
+        def e2_bank(j):
+            eb[2, j] = ps_o.tile([P, PACK, P], F32, name="e2b", tag="o")
+            for t in range(PACK):
+                skew(eb[2, j][:, t, :], j, t, eye, neg)
+
+        def e2_gain(j):
+            nc.vector.tensor_tensor(
+                out=e2g[:, j, :, :], in0=eb[2, j][:].rearrange("p t m -> p m t"),
+                in1=q4[:].unsqueeze(1).to_broadcast([P, P, PACK]), op=MULT,
+            )
+
+        def e1_bank(t):
+            eb[1, t] = ps_u.tile([P, PACK, P], F32, name="e1b", tag="u") if t < 2 else ps_o.tile([P, PACK, P], F32, name="e1b2", tag="o")
+            for j in range(PACK):
+                skew(eb[1, t][:, j, :], j, t, neg, eye)
+
+        def e1_gain(t):
+            nc.scalar.activation(out=e1p[:, t, :], in_=eb[1, t][:].rearrange("p j m -> p (j m)"), func=COPY, scale=p4f[:, t : t + 1])
+
+        def e1_gather():
+            nc.scalar.copy(out=e1g[:], in_=e1p[:].rearrange("p t c -> p c t"))
+
+        vgp = [keep.tile([P, PACK, HALF], BF16, name="vgp_%d" % h) for h in range(2)]
+
+        def vs_bank(h, t):
+            vb[h, t] = ps_o.tile([P, HALF], F32, name="vb", tag="o")
+            mx(vb[h, t][:], e2q, slice(t * P, (t + 1) * P), wq[h], FULL)
+
+        def vs_gain(h, t):
+            nc.scalar.activation(out=vgp[h][:, t, :], in_=vb[h, t][:], func=COPY, scale=gv4f[:, t : t + 1])
+
+        def vs_gather(h):
+            nc.vector.tensor_copy(out=vgb[h][:], in_=vgp[h][:].rearrange("p t f -> p f t"))
+
+        def w_gather(h, eng):
+            if eng == "V":
+                nc.vector.tensor_copy(out=wg[h][:], in_=w4[h][:].rearrange("p t f -> p f t"))
+            else:
+                nc.scalar.copy(out=wg[h][:], in_=w4[h][:].rearrange("p t f -> p f t"))
+
+        def v_bank(h, c):
+            vb[h, c] = ps_o.tile([P, PACK, P], F32, name="vb", tag="o")
+            for t in range(PACK):
+                mx(vb[h, c][:, t, :], e2q, slice(t * P, (t + 1) * P), wq[h], slice(c * P, (c + 1) * P))
+
+        def v_gain(h, c):
+            nc.vector.tensor_tensor(
+                out=vgb[h][:, c * P : (c + 1) * P, :], in0=vb[h, c][:].rearrange("p t f -> p f t"),
+                in1=gv4[:].unsqueeze(1).to_broadcast([P, P, PACK]), op=MULT,
+            )
+
+        def flat(t):
+            return t[:].rearrange("p c t -> p (c t)")
+
+        for j in range(PACK):
+            e2_bank(j)
+        nc.vector.tensor_copy(out=p4f[:], in_=p4[:])
+        nc.vector.tensor_copy(out=gv4f[:], in_=gv4[:])
+        widen(0, 0)
+        widen(0, 1)
+        w_gather(0, "S")
+        e1_bank(0)
+        e1_bank(1)
+        turn(0, 0)
+        turn(0, 1)
+        for j in range(PACK):
+            e2_gain(j)
+        e1_bank(2)
+        e1_bank(3)
+        w_gather(1, "S")
+        for t in range(PACK):
+            e1_gain(t)
+        quant(e2q, FULL, e2g[:].rearrange("p j m t -> p (j m t)"))
+        quant(wq[0], FULL, flat(wg[0]))
+        widen(1, 0)
+        for c in range(4):
+            v_bank(0, c)
+            v_gain(0, c)
+        quant(wq[1], FULL, flat(wg[1]))
+        gather_k(0, 0)
+        gather_k(0, 1)
+        e1_gather()
+        for t in range(4):
+            vs_bank(1, t)
+            vs_gain(1, t)
+        quant(vgq[0], FULL, flat(vgb[0]))
+        quant_x(0)
+        quant_x(1)
+        quant(e1q, FULL, flat(e1g))
+
+        def drain_engine(k, i, h):
+            return "V" if h == 1 and k >= 2 * NB - 2 else "S"
+
+        def first2(k, i):
+            b, h = divmod(k, 2)
+            first(b, 2 * h + i)
+
+        def gain2(k, i):
+            b, h = divmod(k, 2)
+            gain(b, 2 * h + i)
+
+        def out2(k, part):
+            b, h = divmod(k, 2)
+            if not 0 <= b < NB:
+                return
+            order = ((0, 0), (1, 0), (0, 1), (1, 1)) if k == 0 else ((0, 0), (0, 1), (1, 0), (1, 1))
+            for i, f in order[2 * part : 2 * part + 2]:
+                second(b, 2 * h + i, f)
+                leave(b, 2 * h + i, f, drain_engine(k, i, f))
+                if f == 1:
+                    store(b, 2 * h + i)
+
+        def widen2(k):
+            widen(k // 2, k % 2)
+
+        first2(0, 0)
+        first2(0, 1)
+        for k in range(2 * NB + 1):
+            gain2(k, 0)
+            turn((k + 2) // 2, k % 2)
+            gather_k((k + 2) // 2, k % 2)
+            out2(k - 1, 0)
+            first2(k + 1, 0)
+            gain2(k, 1)
+            widen2(k + 3)
+            out2(k - 1, 1)
+            first2(k + 1, 1)
+            quant_u(k // 2, 2 * (k % 2), 2)
+            if k == 0:
+                vs_gather(1)
+                quant(vgq[1], FULL, flat(vgb[1]))
+            quant_x(k + 2)

@@ -68,6 +68,11 @@ def tile_cayleyneumannorthogonallinear_t_kernel(tc, x_bytes, x_scale, a, w0, p, 
         for b0 in range(2, NB, 2):
             load_x(b0, 2)
 
+        blank = keep.tile([P, HALF], BF16, name="blank")
+        nc.gpsimd.memset(blank[:], 0.0)
+        spin = ps_o.tile([P, HALF], F32, name="spin", tag="o")
+        for n in range(5):
+            nc.tensor.matmul(spin[:], lhsT=blank[:, 0:P], rhs=blank[:], start=True, stop=True)
         ident = keep.tile([P, P], F32, name="ident")
         make_identity(nc, ident[:])
         eye = keep.tile([P, P], BF16, name="eye")
@@ -75,6 +80,7 @@ def tile_cayleyneumannorthogonallinear_t_kernel(tc, x_bytes, x_scale, a, w0, p, 
         neg = keep.tile([P, P], BF16, name="neg")
         nc.vector.tensor_scalar(out=neg[:], in0=ident[:], scalar1=-1.0, scalar2=None, op0=MULT)
         p4f = keep.tile([P, PACK], F32, name="p4f")
+        q4f = keep.tile([P, PACK], F32, name="q4f")
         gv4f = keep.tile([P, PACK], F32, name="gv4f")
         warm = keep.tile([P, 1], F32, name="warm")
         nc.vector.memset(warm[:], 1.0)
@@ -86,38 +92,40 @@ def tile_cayleyneumannorthogonallinear_t_kernel(tc, x_bytes, x_scale, a, w0, p, 
             nc.tensor.transpose(bc[:, m, :], s4[:, m : m + 1].to_broadcast([P, P]), ident[:])
         sc = keep.tile([P, 2, P, PACK], F32, name="sc")
         nc.vector.tensor_copy(out=sc[:, 0, :, :], in_=bc[:].rearrange("p m n -> p n m"))
-        nc.scalar.copy(out=sc[:, 1, :, :], in_=bc[:].rearrange("p m n -> p n m"))
+        for r in range(1, 2):
+            nc.scalar.copy(out=sc[:, r, :, :], in_=bc[:].rearrange("p m n -> p n m"))
         sc_flat = sc[:].rearrange("p r n m -> p (r n m)")
 
         xw, xg, xq, ub, ug, uq, xt = {}, {}, {}, {}, {}, {}, {}
 
-        def widen(b, h):
-            if b >= NB:
+        def widen(k, n=1):
+            if k >= 2 * NB:
                 return
-            if h == 0:
-                xw[b] = stage.tile([P, TILES * K], BF16, name="xw", tag="xw")
-            t, i = xb[b]
-            cols = slice(h * 2 * K, (h + 1) * 2 * K)
-            nc.vector.tensor_tensor(out=xw[b][:, cols], in0=t[:, i, cols].bitcast(FP8), in1=sc_flat, op=MULT)
+            tile = stage.tile([P, n * 2 * K], BF16, name="xw%d" % n, tag="xw%d" % n, bufs=8)
+            for j in range(n):
+                xw[k + j] = tile[:, j * 2 * K : (j + 1) * 2 * K]
+            t, i = xb[k // 2]
+            c0 = (k % 2) * 2 * K
+            nc.vector.tensor_tensor(out=tile[:], in0=t[:, i, c0 : c0 + n * 2 * K].bitcast(FP8), in1=sc_flat[:, 0 : n * 2 * K], op=MULT)
 
-        def turn(b, h):
-            if b >= NB:
+        def turn(k):
+            if k >= 2 * NB:
                 return
             bank = ps_x.tile([P, 2, 2, P], F32, name="xt", tag="xt")
-            xt[b, h] = bank
+            xt[k] = bank
             for i in range(2):
-                base = (2 * h + i) * K
-                words = xw[b][:, base : base + K].bitcast(F32)
+                words = xw[k][:, i * K : (i + 1) * K].bitcast(F32)
                 for u in range(2):
                     nc.tensor.transpose(bank[:, i, u, :], words[:, u : K // 2 : 2], ident[:])
 
-        def gather_k(b, h):
-            if b >= NB:
+        def gather_k(k):
+            if k >= 2 * NB:
                 return
+            b, h = divmod(k, 2)
             if h == 0:
-                xg[b] = stage.tile([P, BATCH * PACK], BF16, name="xg", tag="xg", align_bytes=64)
+                xg[b] = stage.tile([P, BATCH * PACK], BF16, name="xg", tag="xg", bufs=5, align_bytes=64)
             words = xg[b][:, h * 2 * K : (h + 1) * 2 * K].bitcast(F32)
-            nc.scalar.copy(out=words.rearrange("p (i r u) -> p i r u", i=2, u=2), in_=xt[b, h][:].rearrange("p i u r -> p i r u"))
+            nc.scalar.copy(out=words.rearrange("p (i r u) -> p i r u", i=2, u=2), in_=xt[k][:].rearrange("p i u r -> p i r u"))
 
         def codes(name, pool, width):
             c = pool.tile([P, width], U32, name=name + "_c", tag=name + "_c", align_bytes=64)
@@ -127,12 +135,18 @@ def tile_cayleyneumannorthogonallinear_t_kernel(tc, x_bytes, x_scale, a, w0, p, 
         def quant(dst, cols, src):
             nc.vector.quantize_mx(out=dst[0][:, cols].bitcast(FP8X4), scales=dst[1][:, cols], in_=src)
 
-        def quant_x(k):
-            b, h = divmod(k, 2)
+        def quant_x(b):
             if b < NB:
-                if h == 0:
-                    xq[b] = codes("xq", stage, BATCH)
-                quant(xq[b], slice(h * 2 * P, (h + 1) * 2 * P), xg[b][:, h * 2 * K : (h + 1) * 2 * K])
+                xq[b] = codes("xq", stage, BATCH)
+                quant(xq[b], slice(0, BATCH), xg[b][:])
+
+        def quant_xh(k):
+            b, h = divmod(k, 2)
+            if b >= NB:
+                return
+            if h == 0:
+                xq[b] = codes("xq", stage, BATCH)
+            quant(xq[b], slice(h * 2 * P, (h + 1) * 2 * P), xg[b][:, h * 2 * K : (h + 1) * 2 * K])
 
         def mx(dst, l, lc, r, rc):
             nc.tensor.matmul_mx(
@@ -167,7 +181,7 @@ def tile_cayleyneumannorthogonallinear_t_kernel(tc, x_bytes, x_scale, a, w0, p, 
         ob, res = {}, {}
 
         def second(b, i, h):
-            if b < 0:
+            if b < 0 or b >= NB:
                 return
             bank = ps_o.tile([P, HALF], F32, name="o", tag="o")
             ob[b, i, h] = bank
@@ -188,13 +202,21 @@ def tile_cayleyneumannorthogonallinear_t_kernel(tc, x_bytes, x_scale, a, w0, p, 
             if b >= 0:
                 nc.sync.dma_start(out=out_v[b, :, i, :], in_=res[b, i][:])
 
+        def g_interleave(dst, src):
+            nc.gpsimd.tensor_scalar(
+                out=dst[:], in0=src[:].rearrange("p t c -> p c t"), scalar1=1.0, scalar2=0.0, op0=MULT, op1=mybir.AluOpType.add
+            )
+
+        def interleave(copy, dst, src):
+            copy(out=dst[:].rearrange("p (c i) t -> p c t i", i=4), in_=src[:].rearrange("p t (c i) -> p c t i", i=4))
+
         def skew(dst, t_out, t_in, first_eye, second_eye):
             nc.tensor.matmul(dst, lhsT=a4[:, t_out, t_in::PACK], rhs=first_eye[:], start=True, stop=False)
             nc.tensor.matmul(dst, lhsT=second_eye[:], rhs=a4[:, t_in, t_out::PACK], start=False, stop=(t_in != t_out))
             if t_in == t_out:
                 nc.tensor.matmul(dst, lhsT=eye[:], rhs=eye[:], start=False, stop=True)
 
-        e2g = keep.tile([P, PACK, P, PACK], BF16, name="e2g", align_bytes=64)
+        e2g = keep.tile([P, K, PACK], BF16, name="e2g", align_bytes=64)
         e2q = codes("e2q", keep, K)
         e1p = keep.tile([P, PACK, K], BF16, name="e1p")
         e1g = keep.tile([P, K, PACK], BF16, name="e1g", align_bytes=64)
@@ -213,7 +235,7 @@ def tile_cayleyneumannorthogonallinear_t_kernel(tc, x_bytes, x_scale, a, w0, p, 
 
         def e2_gain(j):
             nc.vector.tensor_tensor(
-                out=e2g[:, j, :, :], in0=eb[2, j][:].rearrange("p t m -> p m t"),
+                out=e2g[:, j * P : (j + 1) * P, :], in0=eb[2, j][:].rearrange("p t m -> p m t"),
                 in1=q4[:].unsqueeze(1).to_broadcast([P, P, PACK]), op=MULT,
             )
 
@@ -226,9 +248,21 @@ def tile_cayleyneumannorthogonallinear_t_kernel(tc, x_bytes, x_scale, a, w0, p, 
             nc.scalar.activation(out=e1p[:, t, :], in_=eb[1, t][:].rearrange("p j m -> p (j m)"), func=COPY, scale=p4f[:, t : t + 1])
 
         def e1_gather():
-            nc.scalar.copy(out=e1g[:], in_=e1p[:].rearrange("p t c -> p c t"))
+            interleave(nc.scalar.copy, e1g, e1p)
 
+        e2p = keep.tile([P, PACK, K], BF16, name="e2p")
         vgp = [keep.tile([P, PACK, HALF], BF16, name="vgp_%d" % h) for h in range(2)]
+
+        def e2s_bank(t):
+            eb[2, t] = ps_o.tile([P, PACK, P], F32, name="e2b", tag="o")
+            for j in range(PACK):
+                skew(eb[2, t][:, j, :], j, t, eye, neg)
+
+        def e2s_gain(t):
+            nc.scalar.activation(out=e2p[:, t, :], in_=eb[2, t][:].rearrange("p j m -> p (j m)"), func=COPY, scale=q4f[:, t : t + 1])
+
+        def e2s_gather():
+            interleave(nc.vector.tensor_copy, e2g, e2p)
 
         def vs_bank(h, t):
             vb[h, t] = ps_o.tile([P, HALF], F32, name="vb", tag="o")
@@ -238,13 +272,13 @@ def tile_cayleyneumannorthogonallinear_t_kernel(tc, x_bytes, x_scale, a, w0, p, 
             nc.scalar.activation(out=vgp[h][:, t, :], in_=vb[h, t][:], func=COPY, scale=gv4f[:, t : t + 1])
 
         def vs_gather(h):
-            nc.vector.tensor_copy(out=vgb[h][:], in_=vgp[h][:].rearrange("p t f -> p f t"))
+            interleave(nc.vector.tensor_copy, vgb[h], vgp[h])
 
         def w_gather(h, eng):
             if eng == "V":
-                nc.vector.tensor_copy(out=wg[h][:], in_=w4[h][:].rearrange("p t f -> p f t"))
+                interleave(nc.vector.tensor_copy, wg[h], w4[h])
             else:
-                nc.scalar.copy(out=wg[h][:], in_=w4[h][:].rearrange("p t f -> p f t"))
+                interleave(nc.scalar.copy, wg[h], w4[h])
 
         def v_bank(h, c):
             vb[h, c] = ps_o.tile([P, PACK, P], F32, name="vb", tag="o")
@@ -260,81 +294,505 @@ def tile_cayleyneumannorthogonallinear_t_kernel(tc, x_bytes, x_scale, a, w0, p, 
         def flat(t):
             return t[:].rearrange("p c t -> p (c t)")
 
-        for j in range(PACK):
-            e2_bank(j)
+        nc.vector.tensor_copy(out=q4f[:], in_=q4[:])
         nc.vector.tensor_copy(out=p4f[:], in_=p4[:])
         nc.vector.tensor_copy(out=gv4f[:], in_=gv4[:])
-        widen(0, 0)
-        widen(0, 1)
+        widen(0)
+        e2s_bank(0)
+        e2s_bank(1)
+        e2s_gain(0)
+        widen(1)
+        e2s_bank(2)
         w_gather(0, "S")
+        widen(2)
+        e2s_bank(3)
+        turn(0)
+        widen(3)
+        turn(1)
         e1_bank(0)
-        e1_bank(1)
-        turn(0, 0)
-        turn(0, 1)
-        for j in range(PACK):
-            e2_gain(j)
-        e1_bank(2)
-        e1_bank(3)
-        w_gather(1, "S")
-        for t in range(PACK):
-            e1_gain(t)
-        quant(e2q, FULL, e2g[:].rearrange("p j m t -> p (j m t)"))
+        e2s_gain(1)
         quant(wq[0], FULL, flat(wg[0]))
-        widen(1, 0)
-        for c in range(4):
-            v_bank(0, c)
-            v_gain(0, c)
+        e2s_gain(2)
+        e1_bank(1)
+        widen(4)
+        e2s_gain(3)
+        e1_bank(2)
+        w_gather(1, "S")
+        widen(5)
+        e1_bank(3)
+        e2s_gather()
+        e1_gain(0)
+        widen(6)
+        e1_gain(1)
+        e1_gain(2)
+        quant(e2q, FULL, flat(e2g))
+        e1_gain(3)
         quant(wq[1], FULL, flat(wg[1]))
-        gather_k(0, 0)
-        gather_k(0, 1)
+        gather_k(0)
+        widen(7)
+        v_bank(1, 0)
+        gather_k(1)
+        v_bank(1, 1)
+        v_bank(1, 2)
         e1_gather()
-        for t in range(4):
-            vs_bank(1, t)
-            vs_gain(1, t)
-        quant(vgq[0], FULL, flat(vgb[0]))
-        quant_x(0)
-        quant_x(1)
+        v_gain(1, 0)
+        v_bank(1, 3)
+        turn(2)
+        v_gain(1, 1)
+        vs_bank(0, 0)
+        v_gain(1, 2)
+        vs_bank(0, 1)
+        v_gain(1, 3)
+        turn(3)
+        quant_xh(0)
+        vs_bank(0, 2)
+        gather_k(2)
+        quant(vgq[1], FULL, flat(vgb[1]))
+        vs_bank(0, 3)
+        gather_k(3)
+        quant_xh(1)
+        turn(4)
+        quant_xh(2)
+        vs_gain(0, 0)
         quant(e1q, FULL, flat(e1g))
-
-        def drain_engine(k, i, h):
-            return "V" if h == 1 and k >= 2 * NB - 2 else "S"
-
-        def first2(k, i):
-            b, h = divmod(k, 2)
-            first(b, 2 * h + i)
-
-        def gain2(k, i):
-            b, h = divmod(k, 2)
-            gain(b, 2 * h + i)
-
-        def out2(k, part):
-            b, h = divmod(k, 2)
-            if not 0 <= b < NB:
-                return
-            order = ((0, 0), (1, 0), (0, 1), (1, 1)) if k == 0 else ((0, 0), (0, 1), (1, 0), (1, 1))
-            for i, f in order[2 * part : 2 * part + 2]:
-                second(b, 2 * h + i, f)
-                leave(b, 2 * h + i, f, drain_engine(k, i, f))
-                if f == 1:
-                    store(b, 2 * h + i)
-
-        def widen2(k):
-            widen(k // 2, k % 2)
-
-        first2(0, 0)
-        first2(0, 1)
-        for k in range(2 * NB + 1):
-            gain2(k, 0)
-            turn((k + 2) // 2, k % 2)
-            gather_k((k + 2) // 2, k % 2)
-            out2(k - 1, 0)
-            first2(k + 1, 0)
-            gain2(k, 1)
-            widen2(k + 3)
-            out2(k - 1, 1)
-            first2(k + 1, 1)
-            quant_u(k // 2, 2 * (k % 2), 2)
-            if k == 0:
-                vs_gather(1)
-                quant(vgq[1], FULL, flat(vgb[1]))
-            quant_x(k + 2)
+        turn(5)
+        gather_k(4)
+        quant_xh(3)
+        first(0, 0)
+        widen(8)
+        vs_gain(0, 1)
+        first(0, 1)
+        vs_gain(0, 2)
+        turn(6)
+        gain(0, 0)
+        vs_gain(0, 3)
+        gain(0, 1)
+        gather_k(5)
+        first(0, 2)
+        vs_gather(0)
+        gather_k(6)
+        first(0, 3)
+        turn(7)
+        turn(8)
+        quant_u(0, 0, 2)
+        gather_k(7)
+        quant(vgq[0], FULL, flat(vgb[0]))
+        second(0, 0, 1)
+        gather_k(8)
+        gain(0, 2)
+        second(0, 1, 1)
+        leave(0, 0, 1, "S")
+        second(0, 0, 0)
+        gain(0, 3)
+        second(0, 1, 0)
+        leave(0, 1, 1, "S")
+        first(1, 0)
+        quant_xh(4)
+        first(1, 1)
+        leave(0, 0, 0, "S")
+        store(0, 0)
+        quant_u(0, 2, 2)
+        gain(1, 0)
+        second(0, 2, 0)
+        leave(0, 1, 0, "S")
+        store(0, 1)
+        second(0, 2, 1)
+        gain(1, 1)
+        second(0, 3, 0)
+        leave(0, 2, 0, "S")
+        first(1, 2)
+        quant_xh(5)
+        leave(0, 2, 1, "S")
+        store(0, 2)
+        first(1, 3)
+        quant_u(1, 0, 2)
+        second(0, 3, 1)
+        gain(1, 2)
+        leave(0, 3, 0, "S")
+        second(1, 0, 0)
+        second(1, 0, 1)
+        gain(1, 3)
+        leave(0, 3, 1, "S")
+        store(0, 3)
+        first(2, 0)
+        second(1, 1, 0)
+        quant_xh(6)
+        leave(1, 0, 0, "S")
+        first(2, 1)
+        quant_u(1, 2, 2)
+        second(1, 1, 1)
+        gain(2, 0)
+        leave(1, 0, 1, "S")
+        store(1, 0)
+        second(1, 2, 0)
+        gain(2, 1)
+        leave(1, 1, 0, "S")
+        first(2, 2)
+        second(1, 2, 1)
+        quant_xh(7)
+        leave(1, 1, 1, "S")
+        store(1, 1)
+        first(2, 3)
+        quant_u(2, 0, 2)
+        second(1, 3, 0)
+        gain(2, 2)
+        leave(1, 2, 0, "S")
+        second(1, 3, 1)
+        gain(2, 3)
+        leave(1, 2, 1, "S")
+        store(1, 2)
+        first(3, 0)
+        second(2, 0, 0)
+        quant_xh(8)
+        leave(1, 3, 0, "S")
+        first(3, 1)
+        quant_u(2, 2, 2)
+        second(2, 0, 1)
+        gain(3, 0)
+        leave(1, 3, 1, "S")
+        store(1, 3)
+        second(2, 1, 0)
+        gain(3, 1)
+        leave(2, 0, 0, "S")
+        first(3, 2)
+        second(2, 1, 1)
+        widen(9)
+        leave(2, 0, 1, "S")
+        store(2, 0)
+        first(3, 3)
+        second(2, 2, 0)
+        leave(2, 1, 0, "S")
+        second(2, 2, 1)
+        quant_u(3, 0, 2)
+        leave(2, 1, 1, "S")
+        store(2, 1)
+        turn(9)
+        gain(3, 2)
+        leave(2, 2, 0, "S")
+        gain(3, 3)
+        second(2, 3, 0)
+        leave(2, 2, 1, "S")
+        store(2, 2)
+        first(4, 0)
+        widen(10)
+        second(2, 3, 1)
+        leave(2, 3, 0, "S")
+        first(4, 1)
+        second(3, 0, 0)
+        leave(2, 3, 1, "S")
+        store(2, 3)
+        second(3, 0, 1)
+        quant_u(3, 2, 2)
+        second(3, 1, 0)
+        leave(3, 0, 0, "S")
+        gain(4, 0)
+        turn(10)
+        leave(3, 0, 1, "S")
+        store(3, 0)
+        gain(4, 1)
+        second(3, 1, 1)
+        leave(3, 1, 0, "S")
+        widen(11)
+        second(3, 2, 0)
+        second(3, 2, 1)
+        leave(3, 1, 1, "S")
+        store(3, 1)
+        second(3, 3, 0)
+        gather_k(9)
+        quant_u(4, 0, 2)
+        second(3, 3, 1)
+        widen(12)
+        leave(3, 2, 0, "S")
+        turn(11)
+        leave(3, 2, 1, "S")
+        store(3, 2)
+        quant_xh(9)
+        second(4, 0, 0)
+        leave(3, 3, 0, "S")
+        leave(3, 3, 1, "V")
+        store(3, 3)
+        second(4, 0, 1)
+        first(4, 2)
+        gather_k(10)
+        widen(13)
+        first(4, 3)
+        leave(4, 0, 0, "S")
+        second(4, 1, 0)
+        turn(12)
+        leave(4, 0, 1, "S")
+        store(4, 0)
+        quant_xh(10)
+        gain(4, 2)
+        second(4, 1, 1)
+        leave(4, 1, 0, "S")
+        gain(4, 3)
+        first(5, 0)
+        leave(4, 1, 1, "S")
+        store(4, 1)
+        widen(14)
+        first(5, 1)
+        gather_k(11)
+        gather_k(12)
+        turn(13)
+        quant_u(4, 2, 2)
+        quant_xh(11)
+        turn(14)
+        quant_xh(12)
+        gather_k(13)
+        gain(5, 0)
+        second(4, 2, 0)
+        gather_k(14)
+        gain(5, 1)
+        second(4, 2, 1)
+        first(5, 2)
+        leave(4, 2, 0, "S")
+        quant_xh(13)
+        second(4, 3, 0)
+        quant_u(5, 0, 2)
+        first(5, 3)
+        leave(4, 2, 1, "S")
+        store(4, 2)
+        gain(5, 2)
+        second(4, 3, 1)
+        second(5, 0, 0)
+        leave(4, 3, 0, "S")
+        gain(5, 3)
+        second(5, 0, 1)
+        first(6, 0)
+        leave(4, 3, 1, "S")
+        store(4, 3)
+        quant_xh(14)
+        second(5, 1, 0)
+        quant_u(5, 2, 2)
+        first(6, 1)
+        leave(5, 0, 0, "S")
+        gain(6, 0)
+        second(5, 1, 1)
+        leave(5, 0, 1, "S")
+        store(5, 0)
+        second(5, 2, 0)
+        gain(6, 1)
+        first(6, 2)
+        leave(5, 1, 0, "S")
+        second(5, 2, 1)
+        widen(15)
+        first(6, 3)
+        leave(5, 1, 1, "S")
+        store(5, 1)
+        second(5, 3, 0)
+        leave(5, 2, 0, "S")
+        second(5, 3, 1)
+        quant_u(6, 0, 2)
+        turn(15)
+        gain(6, 2)
+        leave(5, 2, 1, "S")
+        store(5, 2)
+        gain(6, 3)
+        leave(5, 3, 0, "S")
+        second(6, 0, 0)
+        first(7, 0)
+        widen(16)
+        leave(5, 3, 1, "S")
+        store(5, 3)
+        second(6, 0, 1)
+        first(7, 1)
+        leave(6, 0, 0, "S")
+        second(6, 1, 0)
+        second(6, 1, 1)
+        quant_u(6, 2, 2)
+        leave(6, 0, 1, "S")
+        store(6, 0)
+        turn(16)
+        gain(7, 0)
+        leave(6, 1, 0, "S")
+        gain(7, 1)
+        second(6, 2, 0)
+        leave(6, 1, 1, "S")
+        store(6, 1)
+        second(6, 2, 1)
+        widen(17)
+        second(6, 3, 0)
+        gather_k(15)
+        second(6, 3, 1)
+        leave(6, 2, 0, "S")
+        quant_u(7, 0, 2)
+        turn(17)
+        leave(6, 2, 1, "S")
+        store(6, 2)
+        quant_xh(15)
+        widen(18)
+        leave(6, 3, 0, "S")
+        first(7, 2)
+        first(7, 3)
+        leave(6, 3, 1, "S")
+        store(6, 3)
+        second(7, 0, 0)
+        gain(7, 2)
+        second(7, 0, 1)
+        gather_k(16)
+        second(7, 1, 0)
+        gain(7, 3)
+        second(7, 1, 1)
+        leave(7, 0, 0, "S")
+        turn(18)
+        quant_xh(16)
+        leave(7, 0, 1, "S")
+        store(7, 0)
+        quant_u(7, 2, 2)
+        first(8, 0)
+        widen(19)
+        leave(7, 1, 0, "S")
+        first(8, 1)
+        second(7, 2, 0)
+        leave(7, 1, 1, "S")
+        store(7, 1)
+        second(7, 2, 1)
+        gain(8, 0)
+        second(7, 3, 0)
+        gather_k(17)
+        second(7, 3, 1)
+        gain(8, 1)
+        leave(7, 2, 0, "S")
+        turn(19)
+        quant_xh(17)
+        leave(7, 2, 1, "S")
+        store(7, 2)
+        quant_u(8, 0, 2)
+        first(8, 2)
+        widen(20)
+        leave(7, 3, 0, "S")
+        first(8, 3)
+        second(8, 0, 0)
+        leave(7, 3, 1, "S")
+        store(7, 3)
+        second(8, 0, 1)
+        gain(8, 2)
+        second(8, 1, 0)
+        gather_k(18)
+        second(8, 1, 1)
+        gain(8, 3)
+        leave(8, 0, 0, "S")
+        turn(20)
+        quant_xh(18)
+        leave(8, 0, 1, "S")
+        store(8, 0)
+        quant_u(8, 2, 2)
+        first(9, 0)
+        widen(21)
+        leave(8, 1, 0, "S")
+        first(9, 1)
+        second(8, 2, 0)
+        leave(8, 1, 1, "S")
+        store(8, 1)
+        second(8, 2, 1)
+        gain(9, 0)
+        second(8, 3, 0)
+        gather_k(19)
+        second(8, 3, 1)
+        gain(9, 1)
+        leave(8, 2, 0, "S")
+        turn(21)
+        quant_xh(19)
+        leave(8, 2, 1, "S")
+        store(8, 2)
+        quant_u(9, 0, 2)
+        first(9, 2)
+        widen(22)
+        leave(8, 3, 0, "S")
+        first(9, 3)
+        leave(8, 3, 1, "S")
+        store(8, 3)
+        second(9, 0, 0)
+        second(9, 0, 1)
+        gain(9, 2)
+        gather_k(20)
+        second(9, 1, 0)
+        second(9, 1, 1)
+        gain(9, 3)
+        leave(9, 0, 0, "S")
+        turn(22)
+        quant_xh(20)
+        leave(9, 0, 1, "S")
+        store(9, 0)
+        quant_u(9, 2, 2)
+        first(10, 0)
+        widen(23)
+        leave(9, 1, 0, "S")
+        first(10, 1)
+        leave(9, 1, 1, "S")
+        store(9, 1)
+        second(9, 2, 0)
+        second(9, 2, 1)
+        gain(10, 0)
+        gather_k(21)
+        second(9, 3, 0)
+        second(9, 3, 1)
+        gain(10, 1)
+        leave(9, 2, 0, "S")
+        turn(23)
+        quant_xh(21)
+        leave(9, 2, 1, "S")
+        store(9, 2)
+        quant_u(10, 0, 2)
+        first(10, 2)
+        leave(9, 3, 0, "V")
+        leave(9, 3, 1, "S")
+        store(9, 3)
+        first(10, 3)
+        gain(10, 2)
+        gather_k(22)
+        second(10, 0, 0)
+        second(10, 0, 1)
+        gain(10, 3)
+        leave(10, 0, 0, "S")
+        second(10, 1, 0)
+        second(10, 1, 1)
+        quant_xh(22)
+        leave(10, 0, 1, "S")
+        store(10, 0)
+        quant_u(10, 2, 2)
+        first(11, 0)
+        leave(10, 1, 0, "S")
+        leave(10, 1, 1, "V")
+        store(10, 1)
+        first(11, 1)
+        gather_k(23)
+        second(10, 2, 0)
+        gain(11, 0)
+        second(10, 2, 1)
+        leave(10, 2, 0, "S")
+        second(10, 3, 0)
+        gain(11, 1)
+        second(10, 3, 1)
+        leave(10, 2, 1, "S")
+        store(10, 2)
+        quant_xh(23)
+        quant_u(11, 0, 2)
+        leave(10, 3, 0, "S")
+        first(11, 2)
+        leave(10, 3, 1, "V")
+        store(10, 3)
+        first(11, 3)
+        second(11, 0, 0)
+        gain(11, 2)
+        second(11, 0, 1)
+        leave(11, 0, 0, "S")
+        second(11, 1, 0)
+        gain(11, 3)
+        second(11, 1, 1)
+        leave(11, 0, 1, "S")
+        store(11, 0)
+        leave(11, 1, 0, "V")
+        leave(11, 1, 1, "S")
+        store(11, 1)
+        quant_u(11, 2, 2)
+        second(11, 2, 0)
+        second(11, 2, 1)
+        leave(11, 2, 0, "V")
+        second(11, 3, 0)
+        leave(11, 2, 1, "S")
+        store(11, 2)
+        second(11, 3, 1)
+        leave(11, 3, 0, "V")
+        leave(11, 3, 1, "S")
+        store(11, 3)

@@ -19,780 +19,399 @@ P = 128
 PACK = 4
 TILES = 4
 BATCH = P * TILES
-NB = T // BATCH
+BATCHES = T // BATCH
+UNITS = 2 * BATCHES
+UNIT_COLS = 2 * K
 HALF = F // 2
+FIRST, LATER = 1, 0
+
+VECTOR, SCALAR, TENSOR, DMA = ENGINES = ("vector", "scalar", "tensor", "dma")
+STEP = {VECTOR: 40, SCALAR: 30, TENSOR: 0, DMA: 0}
+SEEN = {VECTOR: 216, SCALAR: 216, TENSOR: 180, DMA: 2400}
+SWITCH = 120
+BANK = 512
+PASS_128, PASS_512 = 74, 264
+TURN_128 = 126
+CODES = 512
+SIDE = {VECTOR: 1240, SCALAR: 2370}
+ROW_BYTES = 4
+WEIGHTS = -30
+AHEAD = {"gather": 3, "quantize_x": 3, "widen": 6, "leave": 9}
+HELP = 2
+
+
+def list_schedule(steps):
+    missing = {name: len(step[3]) for name, step in steps.items()}
+    followers = {}
+    for name, step in steps.items():
+        for before in step[3]:
+            followers.setdefault(before, []).append(name)
+    ready = {name: 0 for name in steps if missing[name] == 0}
+    seen = {}
+    free = {engine: 0 for engine in ENGINES}
+    last_kind = None
+    order = []
+    while ready:
+        choices = []
+        for number, engine in enumerate(ENGINES):
+            mine = [name for name in ready if engine in steps[name][0]]
+            if mine:
+                start = max(free[engine], min(ready[name] for name in mine))
+                picks = [
+                    (steps[name][4] + (0 if engine == steps[name][0][0] else HELP), name)
+                    for name in mine
+                    if ready[name] <= start
+                ]
+                choices.append((start, number, min(picks)[1]))
+        start, number, name = min(choices)
+        engine = ENGINES[number]
+        kind, weight = steps[name][1:3]
+        end = start + weight + STEP[engine]
+        if engine == TENSOR:
+            end += SWITCH if last_kind not in (None, kind) else 0
+            last_kind = kind
+        free[engine] = end
+        seen[name] = end + SEEN[engine]
+        order.append((name, engine))
+        ready = {other: when for other, when in ready.items() if other != name}
+        for follower in followers.get(name, []):
+            missing[follower] -= 1
+            if missing[follower] == 0:
+                ready[follower] = max(seen[before] for before in steps[follower][3])
+    return order
 
 
 def tile_cayleyneumannorthogonallinear_t_kernel(tc, x_bytes, x_scale, a, w0, p, q, gu, gv, out):
     nc = tc.nc
-    x_v = x_bytes.rearrange("(b p q) o k -> p b (q o k)", p=P, q=TILES)
-    a_v = a.rearrange("o (m t) k -> (o m) t k", t=PACK)
-    w_v = w0.rearrange("o (m t) f -> (o m) t f", t=PACK)
-    out_v = out.rearrange("(b p q) f -> b p q f", p=P, q=TILES)
+    x_view = x_bytes.rearrange("(b p q) o k -> p b (q o k)", p=P, q=TILES)
+    a_view = a.rearrange("o (m t) k -> (o m) t k", t=PACK)
+    w_view = w0.rearrange("o (m t) f -> (o m) t f", t=PACK)
+    out_view = out.rearrange("(b p q) f -> b p q f", p=P, q=TILES)
 
     with ExitStack() as ctx:
         keep = ctx.enter_context(tc.tile_pool(name="keep", bufs=1))
-        stage = ctx.enter_context(tc.tile_pool(name="stage", bufs=3))
-        outs = ctx.enter_context(tc.tile_pool(name="outs", bufs=8))
-        ps_x = ctx.enter_context(tc.psum_pool(name="ps_x", bufs=2))
-        ps_u = ctx.enter_context(tc.psum_pool(name="ps_u", bufs=2))
-        ps_o = ctx.enter_context(tc.psum_pool(name="ps_o", bufs=4))
+        stage = ctx.enter_context(tc.tile_pool(name="stage", bufs=5))
+        results = ctx.enter_context(tc.tile_pool(name="results", bufs=8))
+        turn_banks = ctx.enter_context(tc.psum_pool(name="turn_banks", bufs=2))
+        u_banks = ctx.enter_context(tc.psum_pool(name="u_banks", bufs=2))
+        out_banks = ctx.enter_context(tc.psum_pool(name="out_banks", bufs=4))
         ctx.enter_context(tc.manual_schedule())
 
-        s4 = keep.tile([P, PACK], F32, name="s4")
-        q4 = keep.tile([P, PACK], BF16, name="q4")
-        p4 = keep.tile([P, PACK], BF16, name="p4")
-        gv4 = keep.tile([P, PACK], BF16, name="gv4")
-        gu4 = keep.tile([P, PACK], BF16, name="gu4")
-        nc.scalar.dma_start(out=s4[:], in_=x_scale.rearrange("a o (n m) -> (a o n) m", m=PACK))
-        xb = {}
+        def load_short(vec, dtype, name):
+            tile = keep.tile([P, PACK], dtype, name=name)
+            nc.scalar.dma_start(out=tile[:], in_=vec)
+            return tile
 
-        def load_x(b0, n):
-            t = keep.tile([P, n, TILES * K], U8, name="x_codes_%d" % b0)
-            nc.sync.dma_start(out=t[:], in_=x_v[:, b0 : b0 + n, :])
-            for i in range(n):
-                xb[b0 + i] = (t, i)
+        x_codes = {}
 
+        def load_x(first_batch, count):
+            tile = keep.tile([P, count, TILES * K], U8, name="x_codes_%d" % first_batch)
+            nc.sync.dma_start(out=tile[:], in_=x_view[:, first_batch : first_batch + count, :])
+            for i in range(count):
+                x_codes[first_batch + i] = tile[:, i, :]
+
+        scale4 = load_short(x_scale.rearrange("a o (n t) -> (a o n) t", t=PACK), F32, "scale4")
         load_x(0, 1)
-        for vec, t in ((q, q4), (p, p4), (gv, gv4), (gu, gu4)):
-            nc.scalar.dma_start(out=t[:], in_=vec.rearrange("o (n t) -> (o n) t", t=PACK))
+        q4, p4, gv4, gu4 = [
+            load_short(vec.rearrange("o (n t) -> (o n) t", t=PACK), BF16, name)
+            for vec, name in ((q, "q4"), (p, "p4"), (gv, "gv4"), (gu, "gu4"))
+        ]
         a4 = keep.tile([P, PACK, K], BF16, name="a4")
-        nc.sync.dma_start(out=a4[:], in_=a_v)
-        w4 = []
-        for h in range(2):
-            t = keep.tile([P, PACK, HALF], BF16, name="w4_%d" % h)
-            nc.sync.dma_start(out=t[:], in_=w_v[:, :, h * HALF : (h + 1) * HALF])
-            w4.append(t)
-            if h == 0:
-                load_x(1, 1)
-        for b0 in range(2, NB, 2):
-            load_x(b0, 2)
+        nc.sync.dma_start(out=a4[:], in_=a_view)
+        w4 = [keep.tile([P, PACK, HALF], BF16, name="w4_%d" % half) for half in range(2)]
+        nc.sync.dma_start(out=w4[0][:], in_=w_view[:, :, 0:HALF])
+        load_x(1, 1)
+        nc.sync.dma_start(out=w4[1][:], in_=w_view[:, :, HALF:F])
+        for b in range(2, BATCHES, 2):
+            load_x(b, 2)
 
         blank = keep.tile([P, HALF], BF16, name="blank")
         nc.gpsimd.memset(blank[:], 0.0)
-        spin = ps_o.tile([P, HALF], F32, name="spin", tag="o")
+        unread = out_banks.tile([P, HALF], F32, name="unread", tag="out")
         for n in range(5):
-            nc.tensor.matmul(spin[:], lhsT=blank[:, 0:P], rhs=blank[:], start=True, stop=True)
-        ident = keep.tile([P, P], F32, name="ident")
-        make_identity(nc, ident[:])
+            nc.tensor.matmul(unread[:], lhsT=blank[:, 0:P], rhs=blank[:], start=True, stop=True)
+
+        eye_f32 = keep.tile([P, P], F32, name="eye_f32")
+        make_identity(nc, eye_f32[:])
         eye = keep.tile([P, P], BF16, name="eye")
-        nc.vector.tensor_copy(out=eye[:], in_=ident[:])
-        neg = keep.tile([P, P], BF16, name="neg")
-        nc.vector.tensor_scalar(out=neg[:], in0=ident[:], scalar1=-1.0, scalar2=None, op0=MULT)
-        p4f = keep.tile([P, PACK], F32, name="p4f")
-        q4f = keep.tile([P, PACK], F32, name="q4f")
-        gv4f = keep.tile([P, PACK], F32, name="gv4f")
-        warm = keep.tile([P, 1], F32, name="warm")
-        nc.vector.memset(warm[:], 1.0)
-        warm2 = keep.tile([P, 1], F32, name="warm2")
-        nc.scalar.activation(out=warm2[:], in_=warm[:], func=COPY, scale=2.0)
+        nc.vector.tensor_copy(out=eye[:], in_=eye_f32[:])
+        minus_eye = keep.tile([P, P], BF16, name="minus_eye")
+        nc.vector.tensor_scalar(out=minus_eye[:], in0=eye_f32[:], scalar1=-1.0, scalar2=None, op0=MULT)
+        one = keep.tile([P, 1], F32, name="one")
+        two = keep.tile([P, 1], F32, name="two")
+        nc.vector.memset(one[:], 1.0)
+        nc.scalar.activation(out=two[:], in_=one[:], func=COPY, scale=2.0)
 
-        bc = ps_x.tile([P, PACK, P], F32, name="bc", tag="xt")
-        for m in range(PACK):
-            nc.tensor.transpose(bc[:, m, :], s4[:, m : m + 1].to_broadcast([P, P]), ident[:])
-        sc = keep.tile([P, 2, P, PACK], F32, name="sc")
-        nc.vector.tensor_copy(out=sc[:, 0, :, :], in_=bc[:].rearrange("p m n -> p n m"))
-        for r in range(1, 2):
-            nc.scalar.copy(out=sc[:, r, :, :], in_=bc[:].rearrange("p m n -> p n m"))
-        sc_flat = sc[:].rearrange("p r n m -> p (r n m)")
+        spread = turn_banks.tile([P, PACK, P], F32, name="spread", tag="turn")
+        for t in range(PACK):
+            nc.tensor.transpose(spread[:, t, :], scale4[:, t : t + 1].to_broadcast([P, P]), eye_f32[:])
+        scales = keep.tile([P, 2, P, PACK], F32, name="scales")
+        nc.vector.tensor_copy(out=scales[:, 0, :, :], in_=spread[:].rearrange("p t n -> p n t"))
+        nc.scalar.copy(out=scales[:, 1, :, :], in_=spread[:].rearrange("p t n -> p n t"))
+        scale_row = scales[:].rearrange("p i n t -> p (i n t)")
+        q4_f32, p4_f32, gv4_f32 = [
+            keep.tile([P, PACK], F32, name=name) for name in ("q4_f32", "p4_f32", "gv4_f32")
+        ]
+        for wide, narrow in ((q4_f32, q4), (p4_f32, p4), (gv4_f32, gv4)):
+            nc.vector.tensor_copy(out=wide[:], in_=narrow[:])
 
-        xw, xg, xq, ub, ug, uq, xt = {}, {}, {}, {}, {}, {}, {}
+        def codes(pool, width, name):
+            words = pool.tile([P, width], U32, name=name + "_words", tag=name + "_words", align_bytes=64)
+            scale_bytes = pool.tile([P, width], U8, name=name + "_scales", tag=name + "_scales", align_bytes=64)
+            return words, scale_bytes
 
-        def widen(k, n=1):
-            if k >= 2 * NB:
-                return
-            tile = stage.tile([P, n * 2 * K], BF16, name="xw%d" % n, tag="xw%d" % n, bufs=8)
-            for j in range(n):
-                xw[k + j] = tile[:, j * 2 * K : (j + 1) * 2 * K]
-            t, i = xb[k // 2]
-            c0 = (k % 2) * 2 * K
-            nc.vector.tensor_tensor(out=tile[:], in0=t[:, i, c0 : c0 + n * 2 * K].bitcast(FP8), in1=sc_flat[:, 0 : n * 2 * K], op=MULT)
-
-        def turn(k):
-            if k >= 2 * NB:
-                return
-            bank = ps_x.tile([P, 2, 2, P], F32, name="xt", tag="xt")
-            xt[k] = bank
-            for i in range(2):
-                words = xw[k][:, i * K : (i + 1) * K].bitcast(F32)
-                for u in range(2):
-                    nc.tensor.transpose(bank[:, i, u, :], words[:, u : K // 2 : 2], ident[:])
-
-        def gather_k(k):
-            if k >= 2 * NB:
-                return
-            b, h = divmod(k, 2)
-            if h == 0:
-                xg[b] = stage.tile([P, BATCH * PACK], BF16, name="xg", tag="xg", bufs=5, align_bytes=64)
-            words = xg[b][:, h * 2 * K : (h + 1) * 2 * K].bitcast(F32)
-            nc.scalar.copy(out=words.rearrange("p (i r u) -> p i r u", i=2, u=2), in_=xt[k][:].rearrange("p i u r -> p i r u"))
-
-        def codes(name, pool, width):
-            c = pool.tile([P, width], U32, name=name + "_c", tag=name + "_c", align_bytes=64)
-            s = pool.tile([P, width], U8, name=name + "_s", tag=name + "_s", align_bytes=64)
-            return c, s
-
-        def quant(dst, cols, src):
+        def quantize(dst, cols, src):
             nc.vector.quantize_mx(out=dst[0][:, cols].bitcast(FP8X4), scales=dst[1][:, cols], in_=src)
 
-        def quant_x(b):
-            if b < NB:
-                xq[b] = codes("xq", stage, BATCH)
-                quant(xq[b], slice(0, BATCH), xg[b][:])
+        def flat(tile):
+            return tile[:].rearrange("p c t -> p (c t)")
 
-        def quant_xh(k):
-            b, h = divmod(k, 2)
-            if b >= NB:
-                return
-            if h == 0:
-                xq[b] = codes("xq", stage, BATCH)
-            quant(xq[b], slice(h * 2 * P, (h + 1) * 2 * P), xg[b][:, h * 2 * K : (h + 1) * 2 * K])
-
-        def mx(dst, l, lc, r, rc):
+        def multiply(bank, left, left_cols, right, right_cols):
             nc.tensor.matmul_mx(
-                out=dst, lhsT=l[0][:, lc].bitcast(FP8X4), lhsT_scale=l[1][:, lc],
-                rhs=r[0][:, rc].bitcast(FP8X4), rhs_scale=r[1][:, rc], start=True, stop=True,
-            )
-
-        def first(b, i):
-            if b >= NB:
-                return
-            bank = ps_u.tile([P, PACK, P], F32, name="u", tag="u")
-            ub[b, i] = bank
-            for t in range(PACK):
-                mx(bank[:, t, :], e1q, slice(t * P, (t + 1) * P), xq[b], slice(i * P, (i + 1) * P))
-
-        def gain(b, i):
-            if b >= NB:
-                return
-            if i == 0:
-                ug[b] = stage.tile([P, BATCH, PACK], BF16, name="ug", tag="ug", align_bytes=64)
-                uq[b] = codes("uq", stage, BATCH)
-            nc.vector.tensor_tensor(
-                out=ug[b][:, i * P : (i + 1) * P, :], in0=ub[b, i][:].rearrange("p t r -> p r t"),
-                in1=gu4[:].unsqueeze(1).to_broadcast([P, P, PACK]), op=MULT,
-            )
-
-        def quant_u(b, i0, n):
-            if b < NB:
-                cols = slice(i0 * P, (i0 + n) * P)
-                quant(uq[b], cols, ug[b][:, cols, :].rearrange("p n t -> p (n t)"))
-
-        ob, res = {}, {}
-
-        def second(b, i, h):
-            if b < 0 or b >= NB:
-                return
-            bank = ps_o.tile([P, HALF], F32, name="o", tag="o")
-            ob[b, i, h] = bank
-            mx(bank[:], uq[b], slice(i * P, (i + 1) * P), vgq[h], slice(0, HALF))
-
-        def leave(b, i, h, eng):
-            if b < 0:
-                return
-            if (b, i) not in res:
-                res[b, i] = outs.tile([P, F], F32, name="res", tag="res")
-            cols = slice(h * HALF, (h + 1) * HALF)
-            if eng == "V":
-                nc.vector.tensor_copy(out=res[b, i][:, cols], in_=ob[b, i, h][:])
-            else:
-                nc.scalar.copy(out=res[b, i][:, cols], in_=ob[b, i, h][:])
-
-        def store(b, i):
-            if b >= 0:
-                nc.sync.dma_start(out=out_v[b, :, i, :], in_=res[b, i][:])
-
-        def g_interleave(dst, src):
-            nc.gpsimd.tensor_scalar(
-                out=dst[:], in0=src[:].rearrange("p t c -> p c t"), scalar1=1.0, scalar2=0.0, op0=MULT, op1=mybir.AluOpType.add
+                out=bank,
+                lhsT=left[0][:, left_cols].bitcast(FP8X4),
+                lhsT_scale=left[1][:, left_cols],
+                rhs=right[0][:, right_cols].bitcast(FP8X4),
+                rhs_scale=right[1][:, right_cols],
+                start=True,
+                stop=True,
             )
 
         def interleave(copy, dst, src):
-            copy(out=dst[:].rearrange("p (c i) t -> p c t i", i=4), in_=src[:].rearrange("p t (c i) -> p c t i", i=4))
-
-        def skew(dst, t_out, t_in, first_eye, second_eye):
-            nc.tensor.matmul(dst, lhsT=a4[:, t_out, t_in::PACK], rhs=first_eye[:], start=True, stop=False)
-            nc.tensor.matmul(dst, lhsT=second_eye[:], rhs=a4[:, t_in, t_out::PACK], start=False, stop=(t_in != t_out))
-            if t_in == t_out:
-                nc.tensor.matmul(dst, lhsT=eye[:], rhs=eye[:], start=False, stop=True)
-
-        e2g = keep.tile([P, K, PACK], BF16, name="e2g", align_bytes=64)
-        e2q = codes("e2q", keep, K)
-        e1p = keep.tile([P, PACK, K], BF16, name="e1p")
-        e1g = keep.tile([P, K, PACK], BF16, name="e1g", align_bytes=64)
-        e1q = codes("e1q", keep, K)
-        wg = [keep.tile([P, HALF, PACK], BF16, name="wg_%d" % h, align_bytes=64) for h in range(2)]
-        wq = [codes("wq%d" % h, keep, HALF) for h in range(2)]
-        vgb = [keep.tile([P, HALF, PACK], BF16, name="vgb_%d" % h, align_bytes=64) for h in range(2)]
-        vgq = [codes("vgq%d" % h, keep, HALF) for h in range(2)]
-        eb, vb = {}, {}
-        FULL = slice(0, 512)
-
-        def e2_bank(j):
-            eb[2, j] = ps_o.tile([P, PACK, P], F32, name="e2b", tag="o")
-            for t in range(PACK):
-                skew(eb[2, j][:, t, :], j, t, eye, neg)
-
-        def e2_gain(j):
-            nc.vector.tensor_tensor(
-                out=e2g[:, j * P : (j + 1) * P, :], in0=eb[2, j][:].rearrange("p t m -> p m t"),
-                in1=q4[:].unsqueeze(1).to_broadcast([P, P, PACK]), op=MULT,
+            copy(
+                out=dst[:].rearrange("p (c i) t -> p c t i", i=4),
+                in_=src[:].rearrange("p t (c i) -> p c t i", i=4),
             )
 
-        def e1_bank(t):
-            eb[1, t] = ps_u.tile([P, PACK, P], F32, name="e1b", tag="u") if t < 2 else ps_o.tile([P, PACK, P], F32, name="e1b2", tag="o")
+        def gain(dst, bank, gain4):
+            nc.vector.tensor_tensor(
+                out=dst,
+                in0=bank[:].rearrange("p t c -> p c t"),
+                in1=gain4[:].unsqueeze(1).to_broadcast([P, P, PACK]),
+                op=MULT,
+            )
+
+        ALL = slice(0, 512)
+
+        def block(n):
+            return slice(n * P, (n + 1) * P)
+
+        e_bank = {}
+        e_mid = {e: keep.tile([P, PACK, K], BF16, name="e%d_mid" % e) for e in (1, 2)}
+        e_codes = {e: codes(keep, K, "e%d" % e) for e in (1, 2)}
+        e_side = {e: keep.tile([P, K, PACK], BF16, name="e%d_side" % e, align_bytes=64) for e in (1, 2)}
+
+        def fill_e(e, t):
+            pool, tag = (u_banks, "u") if (e, t) in ((1, 0), (1, 1)) else (out_banks, "out")
+            bank = pool.tile([P, PACK, P], F32, name="e_bank", tag=tag)
+            e_bank[e, t] = bank
+            turned, plain = (minus_eye, eye) if e == 1 else (eye, minus_eye)
             for j in range(PACK):
-                skew(eb[1, t][:, j, :], j, t, neg, eye)
+                dst = bank[:, j, :]
+                nc.tensor.matmul(dst, lhsT=a4[:, j, t::PACK], rhs=turned[:], start=True, stop=False)
+                nc.tensor.matmul(dst, lhsT=plain[:], rhs=a4[:, t, j::PACK], start=False, stop=(j != t))
+                if j == t:
+                    nc.tensor.matmul(dst, lhsT=eye[:], rhs=eye[:], start=False, stop=True)
 
-        def e1_gain(t):
-            nc.scalar.activation(out=e1p[:, t, :], in_=eb[1, t][:].rearrange("p j m -> p (j m)"), func=COPY, scale=p4f[:, t : t + 1])
+        def gain_e(e, t):
+            wide = p4_f32 if e == 1 else q4_f32
+            nc.scalar.activation(
+                out=e_mid[e][:, t, :],
+                in_=e_bank[e, t][:].rearrange("p j m -> p (j m)"),
+                func=COPY,
+                scale=wide[:, t : t + 1],
+            )
 
-        def e1_gather():
-            interleave(nc.scalar.copy, e1g, e1p)
+        w_side = [keep.tile([P, HALF, PACK], BF16, name="w_side_%d" % half, align_bytes=64) for half in range(2)]
+        w_codes = [codes(keep, HALF, "w_%d" % half) for half in range(2)]
+        v_mid = keep.tile([P, PACK, HALF], BF16, name="v_mid")
+        v_side = [keep.tile([P, HALF, PACK], BF16, name="v_side_%d" % half, align_bytes=64) for half in range(2)]
+        v_codes = [codes(keep, HALF, "v_%d" % half) for half in range(2)]
+        v_bank = {}
 
-        e2p = keep.tile([P, PACK, K], BF16, name="e2p")
-        vgp = [keep.tile([P, PACK, HALF], BF16, name="vgp_%d" % h) for h in range(2)]
-
-        def e2s_bank(t):
-            eb[2, t] = ps_o.tile([P, PACK, P], F32, name="e2b", tag="o")
-            for j in range(PACK):
-                skew(eb[2, t][:, j, :], j, t, eye, neg)
-
-        def e2s_gain(t):
-            nc.scalar.activation(out=e2p[:, t, :], in_=eb[2, t][:].rearrange("p j m -> p (j m)"), func=COPY, scale=q4f[:, t : t + 1])
-
-        def e2s_gather():
-            interleave(nc.vector.tensor_copy, e2g, e2p)
-
-        def vs_bank(h, t):
-            vb[h, t] = ps_o.tile([P, HALF], F32, name="vb", tag="o")
-            mx(vb[h, t][:], e2q, slice(t * P, (t + 1) * P), wq[h], FULL)
-
-        def vs_gain(h, t):
-            nc.scalar.activation(out=vgp[h][:, t, :], in_=vb[h, t][:], func=COPY, scale=gv4f[:, t : t + 1])
-
-        def vs_gather(h):
-            interleave(nc.vector.tensor_copy, vgb[h], vgp[h])
-
-        def w_gather(h, eng):
-            if eng == "V":
-                interleave(nc.vector.tensor_copy, wg[h], w4[h])
+        def fill_v(half, n):
+            if half == FIRST:
+                v_bank[half, n] = out_banks.tile([P, PACK, P], F32, name="v_bank", tag="out")
+                for j in range(PACK):
+                    multiply(v_bank[half, n][:, j, :], e_codes[2], block(j), w_codes[half], block(n))
             else:
-                interleave(nc.scalar.copy, wg[h], w4[h])
+                v_bank[half, n] = out_banks.tile([P, HALF], F32, name="v_bank", tag="out")
+                multiply(v_bank[half, n][:], e_codes[2], block(n), w_codes[half], ALL)
 
-        def v_bank(h, c):
-            vb[h, c] = ps_o.tile([P, PACK, P], F32, name="vb", tag="o")
-            for t in range(PACK):
-                mx(vb[h, c][:, t, :], e2q, slice(t * P, (t + 1) * P), wq[h], slice(c * P, (c + 1) * P))
+        def gain_v(half, n):
+            if half == FIRST:
+                gain(v_side[half][:, block(n), :], v_bank[half, n], gv4)
+            else:
+                nc.scalar.activation(
+                    out=v_mid[:, n, :], in_=v_bank[half, n][:], func=COPY, scale=gv4_f32[:, n : n + 1]
+                )
 
-        def v_gain(h, c):
+        x_wide, x_bank, x_side, x_quant = {}, {}, {}, {}
+        u_bank, u_side, u_quant = {}, {}, {}
+        out_bank, result = {}, {}
+
+        def widen(k):
+            x_wide[k] = stage.tile([P, UNIT_COLS], BF16, name="x_wide", tag="x_wide", bufs=8)
+            first = (k % 2) * UNIT_COLS
             nc.vector.tensor_tensor(
-                out=vgb[h][:, c * P : (c + 1) * P, :], in0=vb[h, c][:].rearrange("p t f -> p f t"),
-                in1=gv4[:].unsqueeze(1).to_broadcast([P, P, PACK]), op=MULT,
+                out=x_wide[k][:],
+                in0=x_codes[k // 2][:, first : first + UNIT_COLS].bitcast(FP8),
+                in1=scale_row,
+                op=MULT,
             )
 
-        def flat(t):
-            return t[:].rearrange("p c t -> p (c t)")
+        def turn(k):
+            x_bank[k] = turn_banks.tile([P, 2, 2, P], F32, name="turn", tag="turn")
+            for i in range(2):
+                words = x_wide[k][:, i * K : (i + 1) * K].bitcast(F32)
+                for s in range(2):
+                    nc.tensor.transpose(x_bank[k][:, i, s, :], words[:, s : K // 2 : 2], eye_f32[:])
 
-        nc.vector.tensor_copy(out=q4f[:], in_=q4[:])
-        nc.vector.tensor_copy(out=p4f[:], in_=p4[:])
-        nc.vector.tensor_copy(out=gv4f[:], in_=gv4[:])
-        widen(0)
-        e2s_bank(0)
-        e2s_bank(1)
-        e2s_gain(0)
-        widen(1)
-        e2s_bank(2)
-        w_gather(0, "S")
-        widen(2)
-        e2s_bank(3)
-        turn(0)
-        widen(3)
-        turn(1)
-        e1_bank(0)
-        e2s_gain(1)
-        quant(wq[0], FULL, flat(wg[0]))
-        e2s_gain(2)
-        e1_bank(1)
-        widen(4)
-        e2s_gain(3)
-        e1_bank(2)
-        w_gather(1, "S")
-        widen(5)
-        e1_bank(3)
-        e2s_gather()
-        e1_gain(0)
-        widen(6)
-        e1_gain(1)
-        e1_gain(2)
-        quant(e2q, FULL, flat(e2g))
-        e1_gain(3)
-        quant(wq[1], FULL, flat(wg[1]))
-        gather_k(0)
-        widen(7)
-        v_bank(1, 0)
-        gather_k(1)
-        v_bank(1, 1)
-        v_bank(1, 2)
-        e1_gather()
-        v_gain(1, 0)
-        v_bank(1, 3)
-        turn(2)
-        v_gain(1, 1)
-        vs_bank(0, 0)
-        v_gain(1, 2)
-        vs_bank(0, 1)
-        v_gain(1, 3)
-        turn(3)
-        quant_xh(0)
-        vs_bank(0, 2)
-        gather_k(2)
-        quant(vgq[1], FULL, flat(vgb[1]))
-        vs_bank(0, 3)
-        gather_k(3)
-        quant_xh(1)
-        turn(4)
-        quant_xh(2)
-        vs_gain(0, 0)
-        quant(e1q, FULL, flat(e1g))
-        turn(5)
-        gather_k(4)
-        quant_xh(3)
-        first(0, 0)
-        widen(8)
-        vs_gain(0, 1)
-        first(0, 1)
-        vs_gain(0, 2)
-        turn(6)
-        gain(0, 0)
-        vs_gain(0, 3)
-        gain(0, 1)
-        gather_k(5)
-        first(0, 2)
-        vs_gather(0)
-        gather_k(6)
-        first(0, 3)
-        turn(7)
-        turn(8)
-        quant_u(0, 0, 2)
-        gather_k(7)
-        quant(vgq[0], FULL, flat(vgb[0]))
-        second(0, 0, 1)
-        gather_k(8)
-        gain(0, 2)
-        second(0, 1, 1)
-        leave(0, 0, 1, "S")
-        second(0, 0, 0)
-        gain(0, 3)
-        second(0, 1, 0)
-        leave(0, 1, 1, "S")
-        first(1, 0)
-        quant_xh(4)
-        first(1, 1)
-        leave(0, 0, 0, "S")
-        store(0, 0)
-        quant_u(0, 2, 2)
-        gain(1, 0)
-        second(0, 2, 0)
-        leave(0, 1, 0, "S")
-        store(0, 1)
-        second(0, 2, 1)
-        gain(1, 1)
-        second(0, 3, 0)
-        leave(0, 2, 0, "S")
-        first(1, 2)
-        quant_xh(5)
-        leave(0, 2, 1, "S")
-        store(0, 2)
-        first(1, 3)
-        quant_u(1, 0, 2)
-        second(0, 3, 1)
-        gain(1, 2)
-        leave(0, 3, 0, "S")
-        second(1, 0, 0)
-        second(1, 0, 1)
-        gain(1, 3)
-        leave(0, 3, 1, "S")
-        store(0, 3)
-        first(2, 0)
-        second(1, 1, 0)
-        quant_xh(6)
-        leave(1, 0, 0, "S")
-        first(2, 1)
-        quant_u(1, 2, 2)
-        second(1, 1, 1)
-        gain(2, 0)
-        leave(1, 0, 1, "S")
-        store(1, 0)
-        second(1, 2, 0)
-        gain(2, 1)
-        leave(1, 1, 0, "S")
-        first(2, 2)
-        second(1, 2, 1)
-        quant_xh(7)
-        leave(1, 1, 1, "S")
-        store(1, 1)
-        first(2, 3)
-        quant_u(2, 0, 2)
-        second(1, 3, 0)
-        gain(2, 2)
-        leave(1, 2, 0, "S")
-        second(1, 3, 1)
-        gain(2, 3)
-        leave(1, 2, 1, "S")
-        store(1, 2)
-        first(3, 0)
-        second(2, 0, 0)
-        quant_xh(8)
-        leave(1, 3, 0, "S")
-        first(3, 1)
-        quant_u(2, 2, 2)
-        second(2, 0, 1)
-        gain(3, 0)
-        leave(1, 3, 1, "S")
-        store(1, 3)
-        second(2, 1, 0)
-        gain(3, 1)
-        leave(2, 0, 0, "S")
-        first(3, 2)
-        second(2, 1, 1)
-        widen(9)
-        leave(2, 0, 1, "S")
-        store(2, 0)
-        first(3, 3)
-        second(2, 2, 0)
-        leave(2, 1, 0, "S")
-        second(2, 2, 1)
-        quant_u(3, 0, 2)
-        leave(2, 1, 1, "S")
-        store(2, 1)
-        turn(9)
-        gain(3, 2)
-        leave(2, 2, 0, "S")
-        gain(3, 3)
-        second(2, 3, 0)
-        leave(2, 2, 1, "S")
-        store(2, 2)
-        first(4, 0)
-        widen(10)
-        second(2, 3, 1)
-        leave(2, 3, 0, "S")
-        first(4, 1)
-        second(3, 0, 0)
-        leave(2, 3, 1, "S")
-        store(2, 3)
-        second(3, 0, 1)
-        quant_u(3, 2, 2)
-        second(3, 1, 0)
-        leave(3, 0, 0, "S")
-        gain(4, 0)
-        turn(10)
-        leave(3, 0, 1, "S")
-        store(3, 0)
-        gain(4, 1)
-        second(3, 1, 1)
-        leave(3, 1, 0, "S")
-        widen(11)
-        second(3, 2, 0)
-        second(3, 2, 1)
-        leave(3, 1, 1, "S")
-        store(3, 1)
-        second(3, 3, 0)
-        gather_k(9)
-        quant_u(4, 0, 2)
-        second(3, 3, 1)
-        widen(12)
-        leave(3, 2, 0, "S")
-        turn(11)
-        leave(3, 2, 1, "S")
-        store(3, 2)
-        quant_xh(9)
-        second(4, 0, 0)
-        leave(3, 3, 0, "S")
-        leave(3, 3, 1, "V")
-        store(3, 3)
-        second(4, 0, 1)
-        first(4, 2)
-        gather_k(10)
-        widen(13)
-        first(4, 3)
-        leave(4, 0, 0, "S")
-        second(4, 1, 0)
-        turn(12)
-        leave(4, 0, 1, "S")
-        store(4, 0)
-        quant_xh(10)
-        gain(4, 2)
-        second(4, 1, 1)
-        leave(4, 1, 0, "S")
-        gain(4, 3)
-        first(5, 0)
-        leave(4, 1, 1, "S")
-        store(4, 1)
-        widen(14)
-        first(5, 1)
-        gather_k(11)
-        gather_k(12)
-        turn(13)
-        quant_u(4, 2, 2)
-        quant_xh(11)
-        turn(14)
-        quant_xh(12)
-        gather_k(13)
-        gain(5, 0)
-        second(4, 2, 0)
-        gather_k(14)
-        gain(5, 1)
-        second(4, 2, 1)
-        first(5, 2)
-        leave(4, 2, 0, "S")
-        quant_xh(13)
-        second(4, 3, 0)
-        quant_u(5, 0, 2)
-        first(5, 3)
-        leave(4, 2, 1, "S")
-        store(4, 2)
-        gain(5, 2)
-        second(4, 3, 1)
-        second(5, 0, 0)
-        leave(4, 3, 0, "S")
-        gain(5, 3)
-        second(5, 0, 1)
-        first(6, 0)
-        leave(4, 3, 1, "S")
-        store(4, 3)
-        quant_xh(14)
-        second(5, 1, 0)
-        quant_u(5, 2, 2)
-        first(6, 1)
-        leave(5, 0, 0, "S")
-        gain(6, 0)
-        second(5, 1, 1)
-        leave(5, 0, 1, "S")
-        store(5, 0)
-        second(5, 2, 0)
-        gain(6, 1)
-        first(6, 2)
-        leave(5, 1, 0, "S")
-        second(5, 2, 1)
-        widen(15)
-        first(6, 3)
-        leave(5, 1, 1, "S")
-        store(5, 1)
-        second(5, 3, 0)
-        leave(5, 2, 0, "S")
-        second(5, 3, 1)
-        quant_u(6, 0, 2)
-        turn(15)
-        gain(6, 2)
-        leave(5, 2, 1, "S")
-        store(5, 2)
-        gain(6, 3)
-        leave(5, 3, 0, "S")
-        second(6, 0, 0)
-        first(7, 0)
-        widen(16)
-        leave(5, 3, 1, "S")
-        store(5, 3)
-        second(6, 0, 1)
-        first(7, 1)
-        leave(6, 0, 0, "S")
-        second(6, 1, 0)
-        second(6, 1, 1)
-        quant_u(6, 2, 2)
-        leave(6, 0, 1, "S")
-        store(6, 0)
-        turn(16)
-        gain(7, 0)
-        leave(6, 1, 0, "S")
-        gain(7, 1)
-        second(6, 2, 0)
-        leave(6, 1, 1, "S")
-        store(6, 1)
-        second(6, 2, 1)
-        widen(17)
-        second(6, 3, 0)
-        gather_k(15)
-        second(6, 3, 1)
-        leave(6, 2, 0, "S")
-        quant_u(7, 0, 2)
-        turn(17)
-        leave(6, 2, 1, "S")
-        store(6, 2)
-        quant_xh(15)
-        widen(18)
-        leave(6, 3, 0, "S")
-        first(7, 2)
-        first(7, 3)
-        leave(6, 3, 1, "S")
-        store(6, 3)
-        second(7, 0, 0)
-        gain(7, 2)
-        second(7, 0, 1)
-        gather_k(16)
-        second(7, 1, 0)
-        gain(7, 3)
-        second(7, 1, 1)
-        leave(7, 0, 0, "S")
-        turn(18)
-        quant_xh(16)
-        leave(7, 0, 1, "S")
-        store(7, 0)
-        quant_u(7, 2, 2)
-        first(8, 0)
-        widen(19)
-        leave(7, 1, 0, "S")
-        first(8, 1)
-        second(7, 2, 0)
-        leave(7, 1, 1, "S")
-        store(7, 1)
-        second(7, 2, 1)
-        gain(8, 0)
-        second(7, 3, 0)
-        gather_k(17)
-        second(7, 3, 1)
-        gain(8, 1)
-        leave(7, 2, 0, "S")
-        turn(19)
-        quant_xh(17)
-        leave(7, 2, 1, "S")
-        store(7, 2)
-        quant_u(8, 0, 2)
-        first(8, 2)
-        widen(20)
-        leave(7, 3, 0, "S")
-        first(8, 3)
-        second(8, 0, 0)
-        leave(7, 3, 1, "S")
-        store(7, 3)
-        second(8, 0, 1)
-        gain(8, 2)
-        second(8, 1, 0)
-        gather_k(18)
-        second(8, 1, 1)
-        gain(8, 3)
-        leave(8, 0, 0, "S")
-        turn(20)
-        quant_xh(18)
-        leave(8, 0, 1, "S")
-        store(8, 0)
-        quant_u(8, 2, 2)
-        first(9, 0)
-        widen(21)
-        leave(8, 1, 0, "S")
-        first(9, 1)
-        second(8, 2, 0)
-        leave(8, 1, 1, "S")
-        store(8, 1)
-        second(8, 2, 1)
-        gain(9, 0)
-        second(8, 3, 0)
-        gather_k(19)
-        second(8, 3, 1)
-        gain(9, 1)
-        leave(8, 2, 0, "S")
-        turn(21)
-        quant_xh(19)
-        leave(8, 2, 1, "S")
-        store(8, 2)
-        quant_u(9, 0, 2)
-        first(9, 2)
-        widen(22)
-        leave(8, 3, 0, "S")
-        first(9, 3)
-        leave(8, 3, 1, "S")
-        store(8, 3)
-        second(9, 0, 0)
-        second(9, 0, 1)
-        gain(9, 2)
-        gather_k(20)
-        second(9, 1, 0)
-        second(9, 1, 1)
-        gain(9, 3)
-        leave(9, 0, 0, "S")
-        turn(22)
-        quant_xh(20)
-        leave(9, 0, 1, "S")
-        store(9, 0)
-        quant_u(9, 2, 2)
-        first(10, 0)
-        widen(23)
-        leave(9, 1, 0, "S")
-        first(10, 1)
-        leave(9, 1, 1, "S")
-        store(9, 1)
-        second(9, 2, 0)
-        second(9, 2, 1)
-        gain(10, 0)
-        gather_k(21)
-        second(9, 3, 0)
-        second(9, 3, 1)
-        gain(10, 1)
-        leave(9, 2, 0, "S")
-        turn(23)
-        quant_xh(21)
-        leave(9, 2, 1, "S")
-        store(9, 2)
-        quant_u(10, 0, 2)
-        first(10, 2)
-        leave(9, 3, 0, "V")
-        leave(9, 3, 1, "S")
-        store(9, 3)
-        first(10, 3)
-        gain(10, 2)
-        gather_k(22)
-        second(10, 0, 0)
-        second(10, 0, 1)
-        gain(10, 3)
-        leave(10, 0, 0, "S")
-        second(10, 1, 0)
-        second(10, 1, 1)
-        quant_xh(22)
-        leave(10, 0, 1, "S")
-        store(10, 0)
-        quant_u(10, 2, 2)
-        first(11, 0)
-        leave(10, 1, 0, "S")
-        leave(10, 1, 1, "V")
-        store(10, 1)
-        first(11, 1)
-        gather_k(23)
-        second(10, 2, 0)
-        gain(11, 0)
-        second(10, 2, 1)
-        leave(10, 2, 0, "S")
-        second(10, 3, 0)
-        gain(11, 1)
-        second(10, 3, 1)
-        leave(10, 2, 1, "S")
-        store(10, 2)
-        quant_xh(23)
-        quant_u(11, 0, 2)
-        leave(10, 3, 0, "S")
-        first(11, 2)
-        leave(10, 3, 1, "V")
-        store(10, 3)
-        first(11, 3)
-        second(11, 0, 0)
-        gain(11, 2)
-        second(11, 0, 1)
-        leave(11, 0, 0, "S")
-        second(11, 1, 0)
-        gain(11, 3)
-        second(11, 1, 1)
-        leave(11, 0, 1, "S")
-        store(11, 0)
-        leave(11, 1, 0, "V")
-        leave(11, 1, 1, "S")
-        store(11, 1)
-        quant_u(11, 2, 2)
-        second(11, 2, 0)
-        second(11, 2, 1)
-        leave(11, 2, 0, "V")
-        second(11, 3, 0)
-        leave(11, 2, 1, "S")
-        store(11, 2)
-        second(11, 3, 1)
-        leave(11, 3, 0, "V")
-        leave(11, 3, 1, "S")
-        store(11, 3)
+        def gather(k):
+            b, odd = divmod(k, 2)
+            if b not in x_side:
+                x_side[b] = stage.tile([P, 2 * UNIT_COLS], BF16, name="x_side", tag="x_side", align_bytes=64)
+            words = x_side[b][:, odd * UNIT_COLS : (odd + 1) * UNIT_COLS].bitcast(F32)
+            nc.scalar.copy(
+                out=words.rearrange("p (i n w) -> p i n w", i=2, w=2),
+                in_=x_bank[k][:].rearrange("p i w n -> p i n w"),
+            )
+
+        def quantize_x(k):
+            b, odd = divmod(k, 2)
+            if b not in x_quant:
+                x_quant[b] = codes(stage, BATCH, "x")
+            cols = slice(odd * 2 * P, (odd + 1) * 2 * P)
+            quantize(x_quant[b], cols, x_side[b][:, odd * UNIT_COLS : (odd + 1) * UNIT_COLS])
+
+        def fill_u(n):
+            u_bank[n] = u_banks.tile([P, PACK, P], F32, name="u", tag="u")
+            for j in range(PACK):
+                multiply(u_bank[n][:, j, :], e_codes[1], block(j), x_quant[n // TILES], block(n % TILES))
+
+        def gain_u(n):
+            b, i = divmod(n, TILES)
+            if b not in u_side:
+                u_side[b] = stage.tile([P, BATCH, PACK], BF16, name="u_side", tag="u_side", align_bytes=64)
+                u_quant[b] = codes(stage, BATCH, "u")
+            gain(u_side[b][:, block(i), :], u_bank[n], gu4)
+
+        def quantize_u(k):
+            b, odd = divmod(k, 2)
+            cols = slice(odd * 2 * P, (odd + 1) * 2 * P)
+            quantize(u_quant[b], cols, u_side[b][:, cols, :].rearrange("p n t -> p (n t)"))
+
+        def fill_out(n, half):
+            out_bank[n, half] = out_banks.tile([P, HALF], F32, name="out", tag="out")
+            multiply(out_bank[n, half][:], u_quant[n // TILES], block(n % TILES), v_codes[half], ALL)
+
+        def leave(engine, n, half):
+            if n not in result:
+                result[n] = results.tile([P, F], F32, name="result", tag="result")
+            copy = nc.vector.tensor_copy if engine == VECTOR else nc.scalar.copy
+            copy(out=result[n][:, half * HALF : (half + 1) * HALF], in_=out_bank[n, half][:])
+
+        def store(n):
+            nc.sync.dma_start(out=out_view[n // TILES, :, n % TILES, :], in_=result[n][:])
+
+        steps, calls = {}, {}
+
+        def step(name, engines, weight, after, rank, call):
+            steps[name] = (engines, "turn" if name[0] in ("spread", "turn") else "product", weight, after, rank)
+            calls[name] = call
+
+        loads = [("scale4",), ("x", 0), ("a",), ("w", 0), ("x", 1), ("w", 1)] + [("x", b) for b in range(2, BATCHES)]
+        row_bytes = {"scale4": 3600, "x": TILES * K, "a": 2 * PACK * K, "w": 2 * PACK * HALF}
+        for n, load in enumerate(loads):
+            step(("load",) + load, (DMA,), row_bytes[load[0]] // ROW_BYTES, [], n - 1000, None)
+        step(("spread",), (TENSOR,), PACK * TURN_128, [("load", "scale4")], -1000, None)
+        step(("scales", 0), (VECTOR,), BANK, [("spread",)], -1000, None)
+        step(("scales", 1), (SCALAR,), BANK, [("spread",)], -1000, None)
+
+        for e, engine, copy, rank in (
+            (2, VECTOR, nc.vector.tensor_copy, WEIGHTS),
+            (1, SCALAR, nc.scalar.copy, AHEAD["leave"]),
+        ):
+            for t in range(PACK):
+                before = [("load", "a")] if e == 2 else [("fill_e", 2, 3)] + [("gain_e", 2, t - 2)] * (t >= 2)
+                step(("fill_e", e, t), (TENSOR,), 9 * PASS_128, before, WEIGHTS, lambda engine, e=e, t=t: fill_e(e, t))
+                step(("gain_e", e, t), (SCALAR,), BANK, [("fill_e", e, t)], WEIGHTS, lambda engine, e=e, t=t: gain_e(e, t))
+            step(
+                ("side_e", e), (engine,), SIDE[engine], [("gain_e", e, t) for t in range(PACK)], rank,
+                lambda engine, e=e, copy=copy: interleave(copy, e_side[e], e_mid[e]),
+            )
+            step(
+                ("codes_e", e), (VECTOR,), CODES, [("side_e", e)], WEIGHTS,
+                lambda engine, e=e: quantize(e_codes[e], ALL, flat(e_side[e])),
+            )
+        for half in (FIRST, LATER):
+            step(
+                ("side_w", half), (SCALAR,), SIDE[SCALAR], [("load", "w", half)], WEIGHTS,
+                lambda engine, half=half: interleave(nc.scalar.copy, w_side[half], w4[half]),
+            )
+            step(
+                ("codes_w", half), (VECTOR,), CODES, [("side_w", half)], WEIGHTS,
+                lambda engine, half=half: quantize(w_codes[half], ALL, flat(w_side[half])),
+            )
+            for n in range(PACK):
+                freed = ("gain_e", 2 if n < 2 else 1, n % 2 + 2) if half == FIRST else ("gain_v", FIRST, n)
+                step(
+                    ("fill_v", half, n), (TENSOR,), PACK * PASS_128 if half == FIRST else PASS_512,
+                    [("codes_e", 2), ("codes_w", half), freed], WEIGHTS, lambda engine, half=half, n=n: fill_v(half, n),
+                )
+                step(
+                    ("gain_v", half, n), (VECTOR,) if half == FIRST else (SCALAR,), BANK, [("fill_v", half, n)],
+                    WEIGHTS, lambda engine, half=half, n=n: gain_v(half, n),
+                )
+            done = [("gain_v", half, n) for n in range(PACK)]
+            if half == LATER:
+                step(
+                    ("side_v",), (VECTOR,), SIDE[VECTOR], done, WEIGHTS,
+                    lambda engine: interleave(nc.vector.tensor_copy, v_side[LATER], v_mid),
+                )
+                done = [("side_v",)]
+            step(
+                ("codes_v", half), (VECTOR,), CODES, done, WEIGHTS,
+                lambda engine, half=half: quantize(v_codes[half], ALL, flat(v_side[half])),
+            )
+
+        banks = []
+        for k in range(UNITS):
+            pairs = [(i, half) for i in range(2) for half in range(2)]
+            if k == 0:
+                pairs = [(0, FIRST), (1, FIRST), (0, LATER), (1, LATER)]
+            banks += [(2 * k + i, half) for i, half in pairs]
+            step(
+                ("widen", k), (VECTOR,), UNIT_COLS, [("load", "x", k // 2), ("scales", 0), ("scales", 1)],
+                k + AHEAD["widen"], lambda engine, k=k: widen(k),
+            )
+            freed = ("gather", k - 2) if k >= 2 else ("scales", k)
+            step(("turn", k), (TENSOR,), 4 * TURN_128, [("widen", k), freed], k, lambda engine, k=k: turn(k))
+            step(("gather", k), (SCALAR,), BANK, [("turn", k)], k + AHEAD["gather"], lambda engine, k=k: gather(k))
+            step(
+                ("quantize_x", k), (VECTOR,), CODES // 2, [("gather", k)], k + AHEAD["quantize_x"],
+                lambda engine, k=k: quantize_x(k),
+            )
+            for n in (2 * k, 2 * k + 1):
+                freed = ("gain_u", n - 2) if n >= 2 else ("gain_e", 1, n)
+                before = [("quantize_x", k), ("codes_e", 1), freed]
+                step(("fill_u", n), (TENSOR,), PACK * PASS_128, before, k, lambda engine, n=n: fill_u(n))
+                step(("gain_u", n), (VECTOR,), BANK, [("fill_u", n)], k, lambda engine, n=n: gain_u(n))
+            before = [("gain_u", 2 * k), ("gain_u", 2 * k + 1)]
+            step(("quantize_u", k), (VECTOR,), CODES // 2, before, k, lambda engine, k=k: quantize_u(k))
+        for m, (n, half) in enumerate(banks):
+            k = n // 2
+            freed = ("leave",) + banks[m - 4] if m >= 4 else ("gain_v", LATER, m)
+            before = [("quantize_u", k), ("codes_v", half), freed]
+            step(("fill_out", n, half), (TENSOR,), PASS_512, before, k, lambda engine, n=n, half=half: fill_out(n, half))
+            step(
+                ("leave", n, half), (SCALAR, VECTOR), BANK, [("fill_out", n, half)], k + AHEAD["leave"],
+                lambda engine, n=n, half=half: leave(engine, n, half),
+            )
+        for n in range(2 * UNITS):
+            before = [("leave", n, 0), ("leave", n, 1)]
+            step(("store", n), (DMA,), 4 * F // ROW_BYTES, before, n, lambda engine, n=n: store(n))
+
+        for name, engine in list_schedule(steps):
+            if calls[name] is not None:
+                calls[name](engine)

from contextlib import ExitStack

import concourse.mybir as mybir
from concourse.masks import make_identity

T, K, F = 6144, 512, 1024
FLOPS = 2 * T * K * K + 2 * K * K * F + 2 * T * K * F

F32 = mybir.dt.float32
BF16 = mybir.dt.bfloat16
U32 = mybir.dt.uint32
U8 = mybir.dt.uint8
FP8 = mybir.dt.float8_e4m3fn
FP8X4 = mybir.dt.float8_e4m3fn_x4
MULT = mybir.AluOpType.mult
COPY = mybir.ActivationFunctionType.Copy

P = 128
PACK = 4
TILES = 4
BATCH = P * TILES
BATCHES = T // BATCH
UNITS = 2 * BATCHES
UNIT_COLS = 2 * K
HALF = F // 2
FIRST, LATER = 1, 0

VECTOR, SCALAR, TENSOR, DMA = ENGINES = ("vector", "scalar", "tensor", "dma")
STEP = {VECTOR: 40, SCALAR: 30, TENSOR: 0, DMA: 0}
SEEN = {VECTOR: 216, SCALAR: 216, TENSOR: 180, DMA: 2400}
SWITCH = 120
BANK = 512
PASS_128, PASS_512 = 74, 264
TURN_128 = 126
CODES = 512
SIDE = {VECTOR: 1240, SCALAR: 2370}
ROW_BYTES = 4
WEIGHTS = -30
AHEAD = {"gather": 3, "quantize_x": 3, "widen": 6, "leave": 9}
HELP = 2


def list_schedule(steps):
    missing = {name: len(step[3]) for name, step in steps.items()}
    followers = {}
    for name, step in steps.items():
        for before in step[3]:
            followers.setdefault(before, []).append(name)
    ready = {name: 0 for name in steps if missing[name] == 0}
    seen = {}
    free = {engine: 0 for engine in ENGINES}
    last_kind = None
    order = []
    while ready:
        choices = []
        for number, engine in enumerate(ENGINES):
            mine = [name for name in ready if engine in steps[name][0]]
            if mine:
                start = max(free[engine], min(ready[name] for name in mine))
                picks = [
                    (steps[name][4] + (0 if engine == steps[name][0][0] else HELP), name)
                    for name in mine
                    if ready[name] <= start
                ]
                choices.append((start, number, min(picks)[1]))
        start, number, name = min(choices)
        engine = ENGINES[number]
        kind, weight = steps[name][1:3]
        end = start + weight + STEP[engine]
        if engine == TENSOR:
            end += SWITCH if last_kind not in (None, kind) else 0
            last_kind = kind
        free[engine] = end
        seen[name] = end + SEEN[engine]
        order.append((name, engine))
        ready = {other: when for other, when in ready.items() if other != name}
        for follower in followers.get(name, []):
            missing[follower] -= 1
            if missing[follower] == 0:
                ready[follower] = max(seen[before] for before in steps[follower][3])
    return order


def tile_cayleyneumannorthogonallinear_t_kernel(tc, x_bytes, x_scale, a, w0, p, q, gu, gv, out):
    nc = tc.nc
    x_view = x_bytes.rearrange("(b p q) o k -> p b (q o k)", p=P, q=TILES)
    a_view = a.rearrange("o (m t) k -> (o m) t k", t=PACK)
    w_view = w0.rearrange("o (m t) f -> (o m) t f", t=PACK)
    out_view = out.rearrange("(b p q) f -> b p q f", p=P, q=TILES)

    with ExitStack() as ctx:
        keep = ctx.enter_context(tc.tile_pool(name="keep", bufs=1))
        stage = ctx.enter_context(tc.tile_pool(name="stage", bufs=5))
        results = ctx.enter_context(tc.tile_pool(name="results", bufs=8))
        turn_banks = ctx.enter_context(tc.psum_pool(name="turn_banks", bufs=2))
        u_banks = ctx.enter_context(tc.psum_pool(name="u_banks", bufs=2))
        out_banks = ctx.enter_context(tc.psum_pool(name="out_banks", bufs=4))
        ctx.enter_context(tc.manual_schedule())

        def load_short(vec, dtype, name):
            tile = keep.tile([P, PACK], dtype, name=name)
            nc.scalar.dma_start(out=tile[:], in_=vec)
            return tile

        x_codes = {}

        def load_x(first_batch, count):
            tile = keep.tile([P, count, TILES * K], U8, name="x_codes_%d" % first_batch)
            nc.sync.dma_start(out=tile[:], in_=x_view[:, first_batch : first_batch + count, :])
            for i in range(count):
                x_codes[first_batch + i] = tile[:, i, :]

        scale4 = load_short(x_scale.rearrange("a o (n t) -> (a o n) t", t=PACK), F32, "scale4")
        load_x(0, 1)
        q4, p4, gv4, gu4 = [
            load_short(vec.rearrange("o (n t) -> (o n) t", t=PACK), BF16, name)
            for vec, name in ((q, "q4"), (p, "p4"), (gv, "gv4"), (gu, "gu4"))
        ]
        a4 = keep.tile([P, PACK, K], BF16, name="a4")
        nc.sync.dma_start(out=a4[:], in_=a_view)
        w4 = [keep.tile([P, PACK, HALF], BF16, name="w4_%d" % half) for half in range(2)]
        nc.sync.dma_start(out=w4[0][:], in_=w_view[:, :, 0:HALF])
        load_x(1, 1)
        nc.sync.dma_start(out=w4[1][:], in_=w_view[:, :, HALF:F])
        for b in range(2, BATCHES, 2):
            load_x(b, 2)

        blank = keep.tile([P, HALF], BF16, name="blank")
        nc.gpsimd.memset(blank[:], 0.0)
        unread = out_banks.tile([P, HALF], F32, name="unread", tag="out")
        for n in range(5):
            nc.tensor.matmul(unread[:], lhsT=blank[:, 0:P], rhs=blank[:], start=True, stop=True)

        eye_f32 = keep.tile([P, P], F32, name="eye_f32")
        make_identity(nc, eye_f32[:])
        eye = keep.tile([P, P], BF16, name="eye")
        nc.vector.tensor_copy(out=eye[:], in_=eye_f32[:])
        minus_eye = keep.tile([P, P], BF16, name="minus_eye")
        nc.vector.tensor_scalar(out=minus_eye[:], in0=eye_f32[:], scalar1=-1.0, scalar2=None, op0=MULT)
        one = keep.tile([P, 1], F32, name="one")
        two = keep.tile([P, 1], F32, name="two")
        nc.vector.memset(one[:], 1.0)
        nc.scalar.activation(out=two[:], in_=one[:], func=COPY, scale=2.0)

        spread = turn_banks.tile([P, PACK, P], F32, name="spread", tag="turn")
        for t in range(PACK):
            nc.tensor.transpose(spread[:, t, :], scale4[:, t : t + 1].to_broadcast([P, P]), eye_f32[:])
        scales = keep.tile([P, 2, P, PACK], F32, name="scales")
        nc.vector.tensor_copy(out=scales[:, 0, :, :], in_=spread[:].rearrange("p t n -> p n t"))
        nc.scalar.copy(out=scales[:, 1, :, :], in_=spread[:].rearrange("p t n -> p n t"))
        scale_row = scales[:].rearrange("p i n t -> p (i n t)")
        q4_f32, p4_f32, gv4_f32 = [
            keep.tile([P, PACK], F32, name=name) for name in ("q4_f32", "p4_f32", "gv4_f32")
        ]
        for wide, narrow in ((q4_f32, q4), (p4_f32, p4), (gv4_f32, gv4)):
            nc.vector.tensor_copy(out=wide[:], in_=narrow[:])

        def codes(pool, width, name):
            words = pool.tile([P, width], U32, name=name + "_words", tag=name + "_words", align_bytes=64)
            scale_bytes = pool.tile([P, width], U8, name=name + "_scales", tag=name + "_scales", align_bytes=64)
            return words, scale_bytes

        def quantize(dst, cols, src):
            nc.vector.quantize_mx(out=dst[0][:, cols].bitcast(FP8X4), scales=dst[1][:, cols], in_=src)

        def flat(tile):
            return tile[:].rearrange("p c t -> p (c t)")

        def multiply(bank, left, left_cols, right, right_cols):
            nc.tensor.matmul_mx(
                out=bank,
                lhsT=left[0][:, left_cols].bitcast(FP8X4),
                lhsT_scale=left[1][:, left_cols],
                rhs=right[0][:, right_cols].bitcast(FP8X4),
                rhs_scale=right[1][:, right_cols],
                start=True,
                stop=True,
            )

        def interleave(copy, dst, src):
            copy(
                out=dst[:].rearrange("p (c i) t -> p c t i", i=4),
                in_=src[:].rearrange("p t (c i) -> p c t i", i=4),
            )

        def gain(dst, bank, gain4):
            nc.vector.tensor_tensor(
                out=dst,
                in0=bank[:].rearrange("p t c -> p c t"),
                in1=gain4[:].unsqueeze(1).to_broadcast([P, P, PACK]),
                op=MULT,
            )

        ALL = slice(0, 512)

        def block(n):
            return slice(n * P, (n + 1) * P)

        e_bank = {}
        e_mid = {e: keep.tile([P, PACK, K], BF16, name="e%d_mid" % e) for e in (1, 2)}
        e_codes = {e: codes(keep, K, "e%d" % e) for e in (1, 2)}
        e_side = {e: keep.tile([P, K, PACK], BF16, name="e%d_side" % e, align_bytes=64) for e in (1, 2)}

        def fill_e(e, t):
            pool, tag = (u_banks, "u") if (e, t) in ((1, 0), (1, 1)) else (out_banks, "out")
            bank = pool.tile([P, PACK, P], F32, name="e_bank", tag=tag)
            e_bank[e, t] = bank
            turned, plain = (minus_eye, eye) if e == 1 else (eye, minus_eye)
            for j in range(PACK):
                dst = bank[:, j, :]
                nc.tensor.matmul(dst, lhsT=a4[:, j, t::PACK], rhs=turned[:], start=True, stop=False)
                nc.tensor.matmul(dst, lhsT=plain[:], rhs=a4[:, t, j::PACK], start=False, stop=(j != t))
                if j == t:
                    nc.tensor.matmul(dst, lhsT=eye[:], rhs=eye[:], start=False, stop=True)

        def gain_e(e, t):
            wide = p4_f32 if e == 1 else q4_f32
            nc.scalar.activation(
                out=e_mid[e][:, t, :],
                in_=e_bank[e, t][:].rearrange("p j m -> p (j m)"),
                func=COPY,
                scale=wide[:, t : t + 1],
            )

        w_side = [keep.tile([P, HALF, PACK], BF16, name="w_side_%d" % half, align_bytes=64) for half in range(2)]
        w_codes = [codes(keep, HALF, "w_%d" % half) for half in range(2)]
        v_mid = keep.tile([P, PACK, HALF], BF16, name="v_mid")
        v_side = [keep.tile([P, HALF, PACK], BF16, name="v_side_%d" % half, align_bytes=64) for half in range(2)]
        v_codes = [codes(keep, HALF, "v_%d" % half) for half in range(2)]
        v_bank = {}

        def fill_v(half, n):
            if half == FIRST:
                v_bank[half, n] = out_banks.tile([P, PACK, P], F32, name="v_bank", tag="out")
                for j in range(PACK):
                    multiply(v_bank[half, n][:, j, :], e_codes[2], block(j), w_codes[half], block(n))
            else:
                v_bank[half, n] = out_banks.tile([P, HALF], F32, name="v_bank", tag="out")
                multiply(v_bank[half, n][:], e_codes[2], block(n), w_codes[half], ALL)

        def gain_v(half, n):
            if half == FIRST:
                gain(v_side[half][:, block(n), :], v_bank[half, n], gv4)
            else:
                nc.scalar.activation(
                    out=v_mid[:, n, :], in_=v_bank[half, n][:], func=COPY, scale=gv4_f32[:, n : n + 1]
                )

        x_wide, x_bank, x_side, x_quant = {}, {}, {}, {}
        u_bank, u_side, u_quant = {}, {}, {}
        out_bank, result = {}, {}

        def widen(k):
            x_wide[k] = stage.tile([P, UNIT_COLS], BF16, name="x_wide", tag="x_wide", bufs=8)
            first = (k % 2) * UNIT_COLS
            nc.vector.tensor_tensor(
                out=x_wide[k][:],
                in0=x_codes[k // 2][:, first : first + UNIT_COLS].bitcast(FP8),
                in1=scale_row,
                op=MULT,
            )

        def turn(k):
            x_bank[k] = turn_banks.tile([P, 2, 2, P], F32, name="turn", tag="turn")
            for i in range(2):
                words = x_wide[k][:, i * K : (i + 1) * K].bitcast(F32)
                for s in range(2):
                    nc.tensor.transpose(x_bank[k][:, i, s, :], words[:, s : K // 2 : 2], eye_f32[:])

        def gather(k):
            b, odd = divmod(k, 2)
            if b not in x_side:
                x_side[b] = stage.tile([P, 2 * UNIT_COLS], BF16, name="x_side", tag="x_side", align_bytes=64)
            words = x_side[b][:, odd * UNIT_COLS : (odd + 1) * UNIT_COLS].bitcast(F32)
            nc.scalar.copy(
                out=words.rearrange("p (i n w) -> p i n w", i=2, w=2),
                in_=x_bank[k][:].rearrange("p i w n -> p i n w"),
            )

        def quantize_x(k):
            b, odd = divmod(k, 2)
            if b not in x_quant:
                x_quant[b] = codes(stage, BATCH, "x")
            cols = slice(odd * 2 * P, (odd + 1) * 2 * P)
            quantize(x_quant[b], cols, x_side[b][:, odd * UNIT_COLS : (odd + 1) * UNIT_COLS])

        def fill_u(n):
            u_bank[n] = u_banks.tile([P, PACK, P], F32, name="u", tag="u")
            for j in range(PACK):
                multiply(u_bank[n][:, j, :], e_codes[1], block(j), x_quant[n // TILES], block(n % TILES))

        def gain_u(n):
            b, i = divmod(n, TILES)
            if b not in u_side:
                u_side[b] = stage.tile([P, BATCH, PACK], BF16, name="u_side", tag="u_side", align_bytes=64)
                u_quant[b] = codes(stage, BATCH, "u")
            gain(u_side[b][:, block(i), :], u_bank[n], gu4)

        def quantize_u(k):
            b, odd = divmod(k, 2)
            cols = slice(odd * 2 * P, (odd + 1) * 2 * P)
            quantize(u_quant[b], cols, u_side[b][:, cols, :].rearrange("p n t -> p (n t)"))

        def fill_out(n, half):
            out_bank[n, half] = out_banks.tile([P, HALF], F32, name="out", tag="out")
            multiply(out_bank[n, half][:], u_quant[n // TILES], block(n % TILES), v_codes[half], ALL)

        def leave(engine, n, half):
            if n not in result:
                result[n] = results.tile([P, F], F32, name="result", tag="result")
            copy = nc.vector.tensor_copy if engine == VECTOR else nc.scalar.copy
            copy(out=result[n][:, half * HALF : (half + 1) * HALF], in_=out_bank[n, half][:])

        def store(n):
            nc.sync.dma_start(out=out_view[n // TILES, :, n % TILES, :], in_=result[n][:])

        steps, calls = {}, {}

        def step(name, engines, weight, after, rank, call):
            steps[name] = (engines, "turn" if name[0] in ("spread", "turn") else "product", weight, after, rank)
            calls[name] = call

        loads = [("scale4",), ("x", 0), ("a",), ("w", 0), ("x", 1), ("w", 1)] + [("x", b) for b in range(2, BATCHES)]
        row_bytes = {"scale4": 3600, "x": TILES * K, "a": 2 * PACK * K, "w": 2 * PACK * HALF}
        for n, load in enumerate(loads):
            step(("load",) + load, (DMA,), row_bytes[load[0]] // ROW_BYTES, [], n - 1000, None)
        step(("spread",), (TENSOR,), PACK * TURN_128, [("load", "scale4")], -1000, None)
        step(("scales", 0), (VECTOR,), BANK, [("spread",)], -1000, None)
        step(("scales", 1), (SCALAR,), BANK, [("spread",)], -1000, None)

        for e, engine, copy, rank in (
            (2, VECTOR, nc.vector.tensor_copy, WEIGHTS),
            (1, SCALAR, nc.scalar.copy, AHEAD["leave"]),
        ):
            for t in range(PACK):
                before = [("load", "a")] if e == 2 else [("fill_e", 2, 3)] + [("gain_e", 2, t - 2)] * (t >= 2)
                step(("fill_e", e, t), (TENSOR,), 9 * PASS_128, before, WEIGHTS, lambda engine, e=e, t=t: fill_e(e, t))
                step(("gain_e", e, t), (SCALAR,), BANK, [("fill_e", e, t)], WEIGHTS, lambda engine, e=e, t=t: gain_e(e, t))
            step(
                ("side_e", e), (engine,), SIDE[engine], [("gain_e", e, t) for t in range(PACK)], rank,
                lambda engine, e=e, copy=copy: interleave(copy, e_side[e], e_mid[e]),
            )
            step(
                ("codes_e", e), (VECTOR,), CODES, [("side_e", e)], WEIGHTS,
                lambda engine, e=e: quantize(e_codes[e], ALL, flat(e_side[e])),
            )
        for half in (FIRST, LATER):
            step(
                ("side_w", half), (SCALAR,), SIDE[SCALAR], [("load", "w", half)], WEIGHTS,
                lambda engine, half=half: interleave(nc.scalar.copy, w_side[half], w4[half]),
            )
            step(
                ("codes_w", half), (VECTOR,), CODES, [("side_w", half)], WEIGHTS,
                lambda engine, half=half: quantize(w_codes[half], ALL, flat(w_side[half])),
            )
            for n in range(PACK):
                freed = ("gain_e", 2 if n < 2 else 1, n % 2 + 2) if half == FIRST else ("gain_v", FIRST, n)
                step(
                    ("fill_v", half, n), (TENSOR,), PACK * PASS_128 if half == FIRST else PASS_512,
                    [("codes_e", 2), ("codes_w", half), freed], WEIGHTS, lambda engine, half=half, n=n: fill_v(half, n),
                )
                step(
                    ("gain_v", half, n), (VECTOR,) if half == FIRST else (SCALAR,), BANK, [("fill_v", half, n)],
                    WEIGHTS, lambda engine, half=half, n=n: gain_v(half, n),
                )
            done = [("gain_v", half, n) for n in range(PACK)]
            if half == LATER:
                step(
                    ("side_v",), (VECTOR,), SIDE[VECTOR], done, WEIGHTS,
                    lambda engine: interleave(nc.vector.tensor_copy, v_side[LATER], v_mid),
                )
                done = [("side_v",)]
            step(
                ("codes_v", half), (VECTOR,), CODES, done, WEIGHTS,
                lambda engine, half=half: quantize(v_codes[half], ALL, flat(v_side[half])),
            )

        banks = []
        for k in range(UNITS):
            pairs = [(i, half) for i in range(2) for half in range(2)]
            if k == 0:
                pairs = [(0, FIRST), (1, FIRST), (0, LATER), (1, LATER)]
            banks += [(2 * k + i, half) for i, half in pairs]
            step(
                ("widen", k), (VECTOR,), UNIT_COLS, [("load", "x", k // 2), ("scales", 0), ("scales", 1)],
                k + AHEAD["widen"], lambda engine, k=k: widen(k),
            )
            freed = ("gather", k - 2) if k >= 2 else ("scales", k)
            step(("turn", k), (TENSOR,), 4 * TURN_128, [("widen", k), freed], k, lambda engine, k=k: turn(k))
            step(("gather", k), (SCALAR,), BANK, [("turn", k)], k + AHEAD["gather"], lambda engine, k=k: gather(k))
            step(
                ("quantize_x", k), (VECTOR,), CODES // 2, [("gather", k)], k + AHEAD["quantize_x"],
                lambda engine, k=k: quantize_x(k),
            )
            for n in (2 * k, 2 * k + 1):
                freed = ("gain_u", n - 2) if n >= 2 else ("gain_e", 1, n)
                before = [("quantize_x", k), ("codes_e", 1), freed]
                step(("fill_u", n), (TENSOR,), PACK * PASS_128, before, k, lambda engine, n=n: fill_u(n))
                step(("gain_u", n), (VECTOR,), BANK, [("fill_u", n)], k, lambda engine, n=n: gain_u(n))
            before = [("gain_u", 2 * k), ("gain_u", 2 * k + 1)]
            step(("quantize_u", k), (VECTOR,), CODES // 2, before, k, lambda engine, k=k: quantize_u(k))
        for m, (n, half) in enumerate(banks):
            k = n // 2
            freed = ("leave",) + banks[m - 4] if m >= 4 else ("gain_v", LATER, m)
            before = [("quantize_u", k), ("codes_v", half), freed]
            step(("fill_out", n, half), (TENSOR,), PASS_512, before, k, lambda engine, n=n, half=half: fill_out(n, half))
            step(
                ("leave", n, half), (SCALAR, VECTOR), BANK, [("fill_out", n, half)], k + AHEAD["leave"],
                lambda engine, n=n, half=half: leave(engine, n, half),
            )
        for n in range(2 * UNITS):
            before = [("leave", n, 0), ("leave", n, 1)]
            step(("store", n), (DMA,), 4 * F // ROW_BYTES, before, n, lambda engine, n=n: store(n))

        for name, engine in list_schedule(steps):
            if calls[name] is not None:
                calls[name](engine)
